import numpy as np, ml_dtypes
CORES = [83,85,87,115,117,119]
N = 6
BF = ml_dtypes.bfloat16
def gentries(a):
    return np.ascontiguousarray(a.reshape(8, 16, -1).transpose(0, 2, 1)).reshape(8, -1)
def gtable(e):
    e = np.asarray(e); return np.ascontiguousarray(e.reshape(8, -1, 16).transpose(0, 2, 1)).reshape(128, -1).astype(np.int32)
TT, P, R, S, CAP = 1024, 128, 3, 3, 16
def walk(planes, nbr, x, c):
    A = planes.astype(np.int64).reshape(N, 4, 4, TT).transpose(0, 3, 1, 2).reshape(N * TT, 4, 4); B = nbr.astype(np.int64).transpose(0, 2, 1).reshape(N * TT, 4)
    h = np.concatenate([x.astype(np.int64), np.ones((len(x), 1), np.int64)], 1); c = c.astype(np.int64); w = [c]
    for k in range(R):
        q = c // TT
        for s in range(S):
            v = np.einsum("mfc,mc->mf", A[c], h); face = np.argmin(v, 1)
            c = np.where((c // TT == q) & (np.min(v, 1) < 0), B[c, face], c)
        w.append(c)
    return np.stack(w)
def codes(rng, shape, own):
    r = np.arange(N).reshape(N, 1, 1); q = np.where(rng.random(shape) < own, r, (r + rng.integers(1, N, shape)) % N)
    return q * TT + rng.integers(0, TT, shape)
def mesh(rng, big, lo, hi):
    p = rng.integers(-big, big + 1, (N, 4, 4, TT)); p[:, :, 3] = rng.integers(lo, hi + 1, (N, 4, TT)); return p
def roomy(rng, p):
    h = np.stack([1 + rng.permutation(TT - 2)[:TT // 16] for r in range(N)]); k = h.shape[1]
    for r in range(N):
        u = p[r]; u[:, :3, h[r]] = rng.integers(-255, 256, (4, 3, k)); u[:, 3, h[r]] = rng.integers(3 * 255 * 1023, 2 ** 20 + 1, (4, k))
    return h
def choose(rng, p, h, b, x, c):
    big = int(np.abs(x).max()); r = np.arange(N).reshape(N, 1, 1)
    x = np.concatenate([x, rng.integers(-big, big + 1, (N, 8, P, 3))], 2); c = np.concatenate([c, r * TT + h[r, rng.integers(0, h.shape[1], (N, 8, P))]], 2)
    planes = p.reshape(N, 16, TT).astype(np.int32); m = c.shape[2]
    w = walk(planes, b, x.reshape(-1, 3), c.reshape(-1))[:R].reshape(R, N, 8, m) // TT
    cap = np.where(np.eye(N, dtype=bool), P, CAP); cnt = np.zeros((R, N, 8, N), np.int64); n = np.zeros((N, 8), np.int64); keep = np.zeros((N, 8, m), bool)
    k, i, g = np.ogrid[:R, :N, :8]
    for j in range(m):
        q = w[:, :, :, j]; ok = np.all(cnt[k, i, g, q] < cap[i, q], axis=0) & (n < P)
        cnt[k, i, g, q] += ok; n += ok; keep[:, :, j] = ok
    e = rng.permuted(np.nonzero(keep.reshape(N * 8, m))[1].reshape(N, 8, P), axis=2)
    x = np.take_along_axis(x, e[:, :, :, None], 2); c = np.take_along_axis(c, e, 2)
    return {"planes": planes, "nbr": b.astype(np.int32), "pts": np.ascontiguousarray(x.transpose(0, 1, 3, 2)).reshape(N, 24, P).astype(np.int32), "tet0": np.stack([gtable(u) for u in c])}
def setup_inputs(rng):
    p = mesh(rng, 127, -20000, 60000); h = roomy(rng, p)
    return choose(rng, p, h, codes(rng, (N, 4, TT), 0.6), rng.integers(-255, 256, (N, 8, 3 * P, 3)), codes(rng, (N, 8, 3 * P), 0.5))
def setup_inputs_full(rng):
    p = mesh(rng, 127, -20000, 60000); h = roomy(rng, p); r = np.arange(N).reshape(N, 1, 1); m = (N - 1) * CAP
    q = np.broadcast_to((r + 1 + np.arange(m) // CAP) % N, (N, 8, m)); c = q * TT + h[q, rng.integers(0, h.shape[1], (N, 8, m))]
    c = np.where(np.arange(8).reshape(1, 8, 1) % 2 == 0, c, codes(rng, (N, 8, m), 0.0)); c = np.concatenate([c, codes(rng, (N, 8, 2 * P), 0.8)], 2)
    return choose(rng, p, h, codes(rng, (N, 4, TT), 0.6), rng.integers(-255, 256, (N, 8, m + 2 * P, 3)), c)
def setup_inputs_ties(rng):
    p = mesh(rng, 1, -1, 2)
    p[:, 3] = np.where(rng.random((N, 1, TT)) < 0.5, p[:, 1], p[:, 3]); p[:, 2] = np.where(rng.random((N, 1, TT)) < 0.5, p[:, 0], p[:, 2]); h = roomy(rng, p)
    return choose(rng, p, h, codes(rng, (N, 4, TT), 0.6), rng.integers(-2, 3, (N, 8, 3 * P, 3)), codes(rng, (N, 8, 3 * P), 0.5))
def setup_inputs_few(rng):
    p = mesh(rng, 127, -20000, 60000); h = roomy(rng, p); b = codes(rng, (N, 4, TT), 1.0); q = rng.integers(0, N); b[q] = codes(rng, (N, 4, TT), 0.3)[q]
    c = codes(rng, (N, 8, 3 * P), 1.0); out = []
    for v in (b, c):
        u = rng.random(v.shape); out.append(np.where(u < 0.2, v // TT * TT, np.where(u < 0.4, v // TT * TT + TT - 1, v)))
    b, c = out; x = rng.integers(-255, 256, (N, 8, 3 * P, 3)); one = rng.random((N, 8, 3 * P)) < 0.4
    c = np.where(one, c[:, :, :1], c); x = np.where(one[:, :, :, None], x[:, :, :1], x)
    return choose(rng, p, h, b, x, c)
def setup_inputs_spread(rng):
    def some(bits, top, shape, plus):
        v = np.minimum(np.floor(np.exp2(bits * rng.random(shape))).astype(np.int64), top); v = np.where(rng.random(shape) < 0.125, top, v)
        return np.where(rng.random(shape) < plus, v, -v)
    p = some(10, 1023, (N, 4, 4, TT), 0.5); p[:, :, 3] = some(20, 2 ** 20, (N, 4, TT), 0.75); h = roomy(rng, p)
    return choose(rng, p, h, codes(rng, (N, 4, TT), 0.6), some(10, 1023, (N, 8, 3 * P, 3), 0.5), codes(rng, (N, 8, 3 * P), 0.5))
def points(pts, tet0):
    return pts.reshape(N, 8, 3, P).transpose(0, 1, 3, 2).reshape(-1, 3), np.stack([gentries(a) for a in tet0]).reshape(-1)
def check_inputs(d):
    bad = []; p = d["planes"].astype(np.int64).reshape(N, 4, 4, TT)
    if np.abs(p[:, :, :3]).max() > 1023 or np.abs(p[:, :, 3]).max() > 2 ** 20: bad.append("planes out of range")
    if np.abs(d["pts"].astype(np.int64)).max() > 1023: bad.append("pts out of range")
    for a in ("nbr", "tet0"):
        if d[a].min() < 0 or d[a].max() >= N * TT: bad.append(a + " out of range")
    if bad: return bad
    x, c = points(d["pts"], d["tet0"]); w = walk(d["planes"], d["nbr"], x, c)[:R].reshape(R, N, 8, P) // TT
    for q in range(N):
        n = np.count_nonzero(w == q, axis=3); n[:, q] = 0
        if n.max() > CAP: bad.append("more than CAP points of a group on rank " + str(q))
    return bad
def reference(planes, nbr, pts, tet0):
    x, c = points(pts, tet0); e = walk(planes, nbr, x, c)[R].reshape(N, 8, P)
    return {"y": np.stack([gtable(u) for u in e]).astype(np.float32)}

@@ -1,0 +1,379 @@
+from concourse.bass import DstId, RemoteDMATransfer
+from concourse.mybir import AluOpType, ActivationFunctionType
+
+N, TT, P, R, S = 6, 1024, 128, 3, 3
+OFF = 8
+TOP = TT + OFF
+W = TOP + 8
+BIG = 8388608.0
+HOLD = 32768.0
+
+
+def _s(n, dtype="float32"):
+    return ("sbuf", [128, n], dtype)
+
+
+SCRATCH = {
+    "PW": _s(W, "int32"), "NW": _s(W, "int32"), "T0I": _s(8, "int32"),
+    "P4": _s(32, "int32"), "P4H": _s(32, "float16"), "PD": _s(160, "float16"), "PT": _s(640), "PTH": _s(128),
+    "CI": _s(8, "int32"), "CF": _s(8), "CX": _s(4), "IC": _s(128, "int32"), "ICM": _s(128, "int32"),
+    "MI": _s(128), "IA": _s(128), "ID": _s(128), "IDH": _s(128, "float16"), "UA": _s(128), "UB": _s(128), "UT": _s(128, "bfloat16"),
+    "GS": _s(8), "GSH": _s(8, "float16"), "M48": _s(48), "G48": _s(48), "QC": _s(48), "CV": _s(48), "CJ": _s(48), "CJ0": _s(48),
+    "RKI": _s(40), "RNI": _s(40), "RK": _s(40), "RN": _s(40), "CR": _s(40, "bfloat16"), "ON": _s(128, "bfloat16"), "R5": _s(40), "R6": _s(48),
+    "SV": _s(128), "SEL": _s(128, "float16"), "NI": _s(4), "N6": _s(4, "int32"), "N6F": _s(4), "NM": _s(4), "NG": _s(4), "NK": _s(4),
+    "L6": _s(4, "uint16"), "LR": _s(4, "uint16"), "LA": _s(8, "uint16"), "LD": _s(8, "uint16"), "LT": _s(8, "uint16"),
+    "HL": _s(8, "uint16"), "GL": _s(8, "uint16"), "JL": _s(8, "uint16"),
+    "US": _s(48), "QI": _s(48, "int32"), "OH": _s(48, "bfloat16"), "VV": _s(48), "BT": _s(96, "float16"), "SS": _s(48),
+    "AA": _s(128, "float16"), "AT": _s(128), "T1": _s(12), "T2": _s(12), "CHB": _s(48), "RX": _s(48), "DX": _s(128), "YS": _s(8),
+    "GT": _s(80), "LF": _s(8), "EX": _s(80, "float16"), "GDF": _s(128),
+}
+for _t in "HG":
+    _n = 128 if _t == "H" else 80
+    SCRATCH.update({_t + "P": _s(_n), _t + "N": _s(_n), _t + "PM": _s(40), _t + "E": _s(40), _t + "NE": _s(40), _t + "D1": _s(40),
+                    _t + "Z": _s(40), _t + "D": _s(128, "float16"), _t + "CP": _s(40)})
+for _k in range(R):
+    SCRATCH["MS%d" % _k] = _s(12, "float16")
+    SCRATCH["LM%d" % _k] = _s(10, "float16")
+    SCRATCH["RT%d" % _k] = _s(8)
+    SCRATCH["RL%d" % _k] = _s(8)
+for _k in range(8):
+    SCRATCH["b%d" % _k] = ("psum", [128, 512], "float32")
+
+SEMAPHORES = ["v", "t", "s", "c", "ltet", "lpts", "lpl", "lnb", "sty", "pd", "sent"] + ["rq%d" % k for k in range(R)] + ["rt%d" % k for k in range(R)]
+BANKS = ["b%d" % k for k in range(8)]
+
+
+def slot(owner, other):
+    return other - (1 if other > owner else 0)
+
+
+def engine_split(topo, src, dsts):
+    on = [d for d in dsts if topo.chip(d) == topo.chip(src)]
+    off = [d for d in dsts if topo.chip(d) != topo.chip(src)]
+    eo = topo.engines(src, off[0]) if off else []
+    out = {}
+    for ds, es in ((off, eo), (on, [e for e in topo.engines(src, on[0]) if e not in eo] if on else [])):
+        per = 1
+        while ds and 2 * per * len(ds) <= len(es):
+            per *= 2
+        for i, d in enumerate(ds):
+            out[d] = es[i * per:(i + 1) * per]
+    return out
+
+
+def rank_program(g, core, T, topo):
+    me = T.rank_of(core)
+    if me is None:
+        return
+    cores = list(T.cores)
+    others = [q for q in range(N) if q != me]
+    op = AluOpType
+    act = ActivationFunctionType
+    rel = float(OFF - TT * me)
+
+    queues = {"v": g.vector, "t": g.tensor, "s": g.scalar, "c": g, "y": g.sync}
+    known = {q: {} for q in queues}
+    count = {q: 0 for q in queues}
+    clocks, writers, readers = {}, {}, {}
+
+    def wait(q, s, n):
+        queues[q].wait_ge(T.sem[s], n)
+        for a, b in clocks[(s, n)].items():
+            known[q][a] = max(b, known[q].get(a, 0))
+
+    def need(q, r, w):
+        ev = []
+        for k in r:
+            ev += writers.get(k, [])
+            if k in BANKS:
+                ev += [e for e in readers.get(k, []) if e[0] != q]
+        for k in w:
+            ev += writers.get(k, [])
+            ev += [e for e in readers.get(k, []) if e[0] != q]
+        top = {}
+        for s, n in ev:
+            if not (q == "t" and s == "t"):
+                top[s] = max(n, top.get(s, 0))
+        for s, n in sorted(top.items(), key=lambda e: e[0]):
+            if known[q].get(s, 0) >= n:
+                continue
+            if any(o != s and known[q].get(o, 0) < m and clocks[(o, m)].get(s, 0) >= n for o, m in top.items()):
+                continue
+            wait(q, s, n)
+
+    def do(q, fn, r, w):
+        r, w = r.split(), w.split()
+        need(q, r, w)
+        fn(queues[q]).then_inc(T.sem[q], 1)
+        count[q] += 1
+        ev = (q, count[q])
+        clocks[ev] = dict(known[q])
+        clocks[ev][q] = count[q]
+        for k in r:
+            readers.setdefault(k, []).append(ev)
+        for k in w:
+            writers[k] = [ev]
+            readers[k] = []
+
+    def event(sem, total, w):
+        clocks[(sem, total)] = {sem: total}
+        for k in w.split():
+            writers[k] = [(sem, total)]
+            readers[k] = []
+
+    def dma(q, sem, out, in_, r="", w=""):
+        need(q, r.split(), w.split())
+        queues[q].dma_start(out, in_).then_inc(T.sem[sem], 16)
+
+    def tt(out, a, b, o, r, w):
+        do("v", lambda e: e.tensor_tensor(out=out, in0=a, in1=b, op=o), r, w)
+
+    def ts(out, a, s1, o0, r, w, s2=None, o1=None):
+        if o1 is None:
+            do("v", lambda e: e.tensor_scalar(out, a, s1, None, op0=o0), r, w)
+        else:
+            do("v", lambda e: e.tensor_scalar(out, a, s1, s2, op0=o0, op1=o1), r, w)
+
+    def cp(out, a, r, w):
+        do("v", lambda e: e.tensor_copy(out, a), r, w)
+
+    def fill(ap, x, w):
+        do("v", lambda e: e.memset(ap, x), "", w)
+
+    def sfill(ap, n, x, w):
+        do("s", lambda e: e.activation(ap, T.R6[:, 0:n], act.Copy, bias=x, scale=0.0), "R6", w)
+
+    def scan(out, d0, d1, o0, o1, r, w):
+        do("v", lambda e: e.tensor_tensor_scan(out, d0, d1, 0.0, o0, o1), r, w)
+
+    def mm(out, lhsT, rhs, start, stop, r, w):
+        do("t", lambda e: e.matmul(out, lhsT, rhs, start, stop), r, w)
+
+    def iota(out, pattern, base, cm, w, small=True):
+        if small:
+            do("c", lambda e: e.iota(out, pattern, base, cm, allow_small_or_imprecise_dtypes=True), "", w)
+        else:
+            do("c", lambda e: e.iota(out, pattern, base, cm), "", w)
+
+    split = engine_split(topo, core, [cores[q] for q in others])
+    into = sum(len(engine_split(topo, cores[q], [c for c in cores if c != cores[q]])[core]) for q in others)
+    sent = [0]
+
+    def send(src, dst, sem, r):
+        need("c", r.split(), [])
+        tr = []
+        for q in others:
+            rid, pid = topo.addr(cores[q])[:2]
+            tr.append(RemoteDMATransfer(dst_ids=[DstId(rid=rid, pnc=pid)], dma_engine_mask=sum(1 << e for e in split[cores[q]]),
+                                        remote_sem=T.sem[sem], src=src(q), dst=dst(q)))
+            sent[0] += len(split[cores[q]])
+        g.remote_dma_fused(tr, local_sem=T.sem.sent)
+
+    fill(T.P4[:, :], 0, "P4")
+    dma("y", "ltet", T.T0I[:, :], T.tet0[:, :])
+    for b in range(4):
+        dma("y" if b % 2 else "s", "lpts", T.P4[32 * b:32 * b + 24, :], T.pts[:, 32 * b:32 * b + 32], "", "P4")
+    for k in range(8):
+        dma("y" if k % 2 else "s", "lpl", T.PW[16 * k:16 * k + 16, OFF:OFF + TT], T.planes[:, :])
+
+    iota(T.CI[:, 0:1], [[0, 1]], 0, 1, "CI0", small=False)
+    iota(T.IC[:, :], [[1, 128]], 0, 0, "IC", small=False)
+    iota(T.QC[:, :], [[0, 8], [1, 6]], 0, 0, "QC")
+    iota(T.SV[:, :], [[3, 8], [0, 4], [1, 4]], 0, 0, "SV")
+    iota(T.NW[:, 0:W // 2], [[1, W // 2]], 0, 0, "NWc", small=False)
+    event("ltet", 16, "T0I")
+    event("lpts", 64, "P4")
+    event("lpl", 128, "PWa")
+
+    fill(T.US[:, :], 0.0, "US")
+    fill(T.R6[:, :], 1.0, "R6")
+    fill(T.R6[:, 0::6], 0.0, "R6")
+    for ap, n, x, w in ((T.HCP[:, :], 40, rel, "HCP"), (T.GCP[:, :], 40, rel, "GCP"), (T.GZ[:, :], 40, 0.0, "GZ"), (T.R5[:, :], 40, -BIG, "R5"),
+                        (T.R5[:, 0::5], 8, BIG, "R5"), (T.CR[:, :], 40, 0.0, "CR"), (T.CR[:, 0::5], 8, -0.5, "CR")):
+        sfill(ap, n, x, w)
+    rs, an = op.arith_shift_right, op.bitwise_and
+    ts(T.CI[:, 1:2], T.CI[:, 0:1], 15, an, "CI0", "CI1")
+    ts(T.CI[:, 2:3], T.CI[:, 0:1], 4, rs, "CI0", "CI2")
+    ts(T.CI[:, 3:4], T.CI[:, 0:1], 2, rs, "CI0", "CI3")
+    ts(T.CI[:, 4:5], T.CI[:, 0:1], 4, rs, "CI0", "CI4", 1, an)
+    ts(T.CI[:, 5:6], T.CI[:, 0:1], 3, an, "CI0", "CI5")
+    ts(T.CI[:, 6:7], T.CI[:, 0:1], 5, rs, "CI0", "CI6")
+    ts(T.CI[:, 7:8], T.CI[:, 0:1], 31, an, "CI0", "CI7")
+    ts(T.ICM[:, :], T.IC[:, :], 15, an, "IC", "ICM")
+    cp(T.CF[:, :], T.CI[:, :], "CI0 CI1 CI2 CI3 CI4 CI5 CI6 CI7", "CF")
+    p, p15, pg, p2, podd, p3, p5, p31 = [T.CF[:, k:k + 1] for k in range(8)]
+    cp(T.LT[:, :], T.IC[:, 0:8], "IC", "LT")
+    ts(T.MI[:, :], T.ICM[:, :], p15, op.is_equal, "ICM CF", "MI")
+    ts(T.GS[:, :], T.IC[:, 0:8], pg, op.is_equal, "IC CF", "GS")
+    ts(T.NI[:, 0:3], T.IC[:, 0:3], 16.0, op.mult, "IC CF", "NI", p15, op.add)
+    ts(T.UB[:, :], T.IC[:, :], p, op.is_equal, "IC CF", "UB", 256.0, op.mult)
+    ts(T.N6[:, 0:3], T.NI[:, 0:3], 1.0 / 6, op.mult, "NI", "N6", -2.5 / 6, op.add)
+    ts(T.UA[:, :], T.IC[:, :], p, op.is_gt, "IC CF", "UA")
+    ts(T.L6[:, 0:3], T.N6[:, 0:3], 6.0, op.mult, "N6", "L6", 5.0, op.add)
+    tt(T.UT[:, :], T.UA[:, :], T.UB[:, :], op.add, "UA UB", "UT")
+    fill(T.NW[:, W // 2:W], 0, "NWv")
+
+    cp(T.P4H[:, :], T.P4[:, :], "P4", "P4H")
+    send(lambda q: T.P4H[:, :], lambda q: T.PD[:, 32 * slot(q, me):32 * slot(q, me) + 32], "pd", "P4H")
+    event("pd", into, "PD")
+
+    for k in range(8):
+        dma("y", "lnb", T.NW[16 * k:16 * k + 4, OFF:OFF + TT], T.nbr[:, :], "", "NWc NWv")
+    event("lnb", 128, "NWa")
+
+    tt(T.DX[:, :], T.T0I[:, :].indirect(T.LT[:, 0:8]), T.MI[:, :], op.mult, "T0I LT MI", "DX")
+    mm(T.b7[:, 0:8], T.DX[:, :], T.GS[:, :], True, True, "DX GS", "b7")
+    ts(T.CV[:, :], T.QC[:, :], float(-TT), op.mult, "QC", "CV", float(OFF), op.add)
+    ts(T.CX[:, 0:1], p5, 160.0, op.mult, "CF", "CX0", p31, op.add)
+    ts(T.CJ0[:, :], T.QC[:, :], float(me), op.is_lt, "QC", "CJ0", -32.0, op.mult)
+    ts(T.CX[:, 1:2], podd, -1.0, op.mult, "CF", "CX1", 1.0, op.add)
+    cp(T.US[:, 5::6], T.b7[:, 0:8], "b7", "US")
+    ts(T.LA[:, :], T.IC[:, 0:8], 6.0, op.mult, "IC", "LA", 5.0, op.add)
+    ts(T.CJ[:, :], T.CJ0[:, :], T.CX[:, 0:1], op.add, "CJ0 CX0", "CJ", 32.0 * me, op.add)
+
+    def dispatch(k, extra=None):
+        ms = "MS%d" % k
+        ts(T.QI[:, :], T.US[:, :], 1.0 / TT, op.mult, "US", "QI", -0.4995, op.add)
+        tt(T.OH[:, :], T.QI[:, :].indirect(T.L6[:, 0:3]), T.QC[:, :], op.is_equal, "QI L6 QC", "OH")
+        mm(T.b7[:, 0:48], T.UT[:, :], T.OH[:, :], True, True, "UT OH", "b7")
+        tt(T.VV[:, :], T.US[:, :].indirect(T.L6[:, 0:3]), T.CV[:, :], op.add, "US L6 CV", "VV")
+        if extra:
+            extra()
+        scan(T.SS[:, :], T.R6[:, :], T.b7[:, 0:48], op.mult, op.max, "R6 b7", "SS")
+        tt(T.BT[:, 1::2], T.CJ[:, :], T.OH[:, :], op.mult, "CJ OH", "BTj")
+        tt(T.BT[:, 0::2], T.VV[:, :], T.OH[:, :], op.mult, "VV OH", "BTt")
+        tt(T.AA[:, :], T.SS[:, :].indirect(T.LA[:, 0:8]), T.IA[:, :], op.is_equal, "SS LA IA", "AA")
+        for a in range(4):
+            mm(T.b7[32 * a:32 * a + 32, 64:88], T.AA[:, 32 * a:32 * a + 32], T.BT[:, 24 * a:24 * a + 24], True, True, "AA BTj BTt", "b7")
+        ts(T.T1[:, :], T.b7[:, 64:76], T.CX[:, 1:2], op.mult, "b7 CX1", "T1")
+        ts(T.T2[:, :], T.b7[:, 76:88], podd, op.mult, "b7 CF", "T2")
+        tt(T[ms][:, :], T.T1[:, :], T.T2[:, :], op.add, "T1 T2", ms)
+        send(lambda q: T[ms][:, 2 * q:2 * q + 2], lambda q: T["LM%d" % k][:, 2 * slot(q, me):2 * slot(q, me) + 2], "rq%d" % k, ms)
+        event("rq%d" % k, into, "LM%d" % k)
+
+    def hold():
+        mm(T.b6[:, 0:128], T.AA[:, :], T.IDH[:, :], True, True, "AA IDH", "b6")
+        ts(T.CHB[:, :], T.OH[:, :], HOLD, op.mult, "OH", "CHB", -HOLD, op.add)
+        ts(T.CHB[:, me::6], T.OH[:, me::6], HOLD, op.mult, "OH CHB", "CHB", -HOLD - rel, op.add)
+        ts(T.HCP[:, 0::5], T.US[:, 5::6], rel, op.add, "US", "HCP")
+        do("s", lambda e: e.activation(T.AT[:, :], T.b6[:, 0:128], act.Copy), "b6", "AT")
+
+    def step(h, last, between=None):
+        n, lst, pt, bk, bn, bc = (128, T.HL[:, 0:8], "PTH", "b3", "b4", "b5") if h == "H" else (80, T.GL[:, 0:5], "GT", "b0", "b1", "b2")
+        ln, m = h + "L", n // 16
+        X = lambda a: T[h + a]
+        mm(T[bk][0:n, 0:40], T.ON[0:1, 0:n], T.CR[0:1, :], True, False, "ON CR", bk)
+        mm(T[bn][0:n, 0:40], T.ID[0:n, 0:n], X("CP")[0:n, :], True, False, "ID " + h + "CP", bn)
+        tt(X("P")[:, :], T.PW[:, :].indirect(lst), T[pt][:, 0:n], op.mult, "PWa PWb " + ln + " " + pt, h + "P")
+        mm(T[bk][0:n, 0:40], X("P")[:, :], T.RK[:, :], False, True, h + "P RK", bk)
+        cp(X("N")[:, :], T.NW[:, :].indirect(lst), "NWc NWv NWa " + ln, h + "N")
+        mm(T[bn][0:n, 0:40], X("N")[:, :], T.RN[:, :], False, True, h + "N RN", bn)
+        if between:
+            between()
+        scan(X("PM")[0:n, :], T.R5[0:n, :], T[bk][0:n, 0:40], op.max, op.min, "R5 " + bk, h + "PM")
+        tt(X("E")[0:n, :], X("PM")[0:n, :], T[bk][0:n, 0:40], op.is_equal, h + "PM " + bk, h + "E")
+        tt(X("NE")[0:n, :], X("PM")[0:n, :], T[bk][0:n, 0:40], op.not_equal, h + "PM " + bk, h + "NE")
+        tt(X("D1")[0:n, :], X("E")[0:n, :], T[bn][0:n, 0:40], op.mult, h + "E " + bn, h + "D1")
+        scan(X("Z")[0:n, :], X("NE")[0:n, :], X("D1")[0:n, :], op.mult, op.add, h + "NE " + h + "D1", h + "Z")
+        if not last:
+            tt(X("D")[:, :], X("Z")[:, :].indirect(T.LD[:, 0:8]), T.MI[:, :], op.mult, h + "Z LD MI", h + "D")
+            mm(T[bc][:, 0:m], X("D")[0:n, :], T.GSH[0:n, 0:m], True, True, h + "D GSH", bc)
+            cp(X("CP")[0:n, 0::5], X("Z")[0:n, 4::5], h + "Z", h + "CP")
+            ts(lst, T[bc][:, 0:m], float(TOP), op.min, bc, ln)
+        elif h == "H":
+            tt(T.CHB[:, me::6], T.CHB[:, me::6], T.HZ[:, 4::5], op.add, "CHB HZ", "CHB")
+        else:
+            tt(T.GDF[:, :], T.GZ[:, :].indirect(T.LD[:, 0:8]), T.MI[:, :], op.mult, "GZ LD MI", "GDF")
+            mm(T[bc][:, 0:m], T.GDF[0:n, :], T.GS[0:n, 0:m], True, True, "GDF GS", bc)
+
+    def guests(k):
+        lm = "LM%d" % k
+        cp(T.JL[:, 0:5], T[lm][:, 1::2], lm, "JL")
+        do("s", lambda e: e.activation(T.GT[:, :], T.PT[:, :].indirect(T.JL[:, 0:5]), act.Copy), "PT0 PT1 PT2 PT3 JL", "GT")
+        cp(T.LF[:, 0:5], T[lm][:, 0::2], lm, "LF")
+        ts(T.GL[:, 0:5], T[lm][:, 0::2], float(TOP), op.min, lm, "GL")
+        tt(T.EX[:, :], T.LF[:, 0:5].indirect(T.LT[:, 0:5]), T.MI[:, 0:80], op.mult, "LF LT MI", "EX")
+        mm(T.b2[0:80, 0:8], T.EX[:, :], T.GSH[:, :], True, True, "EX GSH", "b2")
+        cp(T.GCP[0:80, 0::5], T.b2[0:80, 0:8], "b2", "GCP")
+        for i in range(S):
+            step("G", i == S - 1)
+        ts(T["RT%d" % k][:, 0:5], T.b2[:, 0:5], -rel, op.add, "b2", "RT%d" % k)
+        send(lambda q: T["RT%d" % k][:, slot(me, q):slot(me, q) + 1], lambda q: T["RL%d" % k][:, slot(q, me):slot(q, me) + 1], "rt%d" % k, "RT%d" % k)
+        event("rt%d" % k, into, "RL%d" % k)
+
+    def replies(k):
+        mm(T.b7[:, 128:176], T.ID[:, :], T.CHB[:, :], True, False, "ID CHB", "b7")
+        tt(T.RX[:, :], T["RL%d" % k][:, 0:5].indirect(T.LR[:, 0:3]), T.M48[:, :], op.mult, "RL%d LR M48" % k, "RX")
+        mm(T.b7[:, 128:176], T.AT[:, :], T.RX[:, :], False, True, "AT RX", "b7")
+        scan(T.US[:, :], T.R6[:, :], T.b7[:, 128:176], op.mult, op.max, "R6 b7", "US")
+
+    def to_list():
+        tt(T.DX[:, :], T.US[:, :].indirect(T.LA[:, 0:8]), T.MI[:, :], op.mult, "US LA MI", "DX")
+        mm(T.b5[:, 0:8], T.DX[:, :], T.GS[:, :], True, True, "DX GS", "b5")
+
+    def spread(bank, at, n, src, b):
+        mm(T[bank][:, at:at + n], T.SEL[32 * b:32 * b + 32, :], T[src][32 * b:32 * b + 32, :], True, True, src + " SEL", bank)
+
+    def guest_points():
+        for b, bank in enumerate(("b0", "b1", "b2", "b6")):
+            spread(bank, 0, 160, "PD", b)
+        for b, bank in enumerate(("b0", "b1", "b2", "b6")):
+            do("s", lambda e: e.activation(T.PT[:, 160 * b:160 * b + 160], T[bank][:, 0:160], act.Identity, bias=T.CX[:, 2:3]), bank + " CX2", "PT%d" % b)
+
+    dispatch(0, lambda: ts(T.IA[:, :], T.ICM[:, :], 256.0, op.add, "ICM", "IA"))
+    iota(T.RKI[:, :], [[4, 8], [-1, 5]], 4, 0, "RKI")
+    iota(T.RNI[:, :], [[16, 8], [-1, 5]], 4, 0, "RNI")
+    iota(T.G48[:, :], [[1, 8], [0, 6]], 0, 0, "G48")
+
+    fill(T.SV[:, 3::4], -1000.0, "SV")
+    ts(T.SEL[:, :], T.SV[:, :], p31, op.is_equal, "SV CF", "SEL")
+    for b in range(4):
+        if b:
+            wait("t", "t", count["t"])
+        spread("b3", 32 * b, 32, "P4H", b)
+    ts(T.CX[:, 2:3], p3, 3.0, op.is_equal, "CF", "CX2")
+    do("s", lambda e: e.activation(T.PTH[:, :], T.b3[:, 0:128], act.Identity, bias=T.CX[:, 2:3]), "b3 CX2", "PTH")
+    ts(T.IDH[:, :], T.IC[:, :], p, op.is_equal, "IC CF", "IDH")
+    ts(T.ID[:, :], T.IC[:, :], p, op.is_equal, "IC CF", "ID")
+    fill(T.PW[:, 0:OFF], 0, "PWb")
+    fill(T.PW[:, TOP:W], 0, "PWb")
+    fill(T.ON[:, :], 1.0, "ON")
+    cp(T.GSH[:, :], T.GS[:, :], "GS", "GSH")
+    ts(T.LD[:, :], T.IC[:, 0:8], 5.0, op.mult, "IC", "LD", 4.0, op.add)
+    ts(T.HL[:, :], T.T0I[:, :], rel, op.add, "T0I", "HL", float(TOP), op.min)
+    hold()
+    ts(T.RK[:, :], T.RKI[:, :], p2, op.is_equal, "RKI CF", "RK")
+    fill(T.RK[:, 0::5], 0.0, "RK")
+    ts(T.RN[:, :], T.RNI[:, :], p, op.is_equal, "RNI CF", "RN")
+    fill(T.RN[:, 0::5], 0.0, "RN")
+
+    for k in range(R):
+        if k:
+            hold()
+            to_list()
+            ts(T.HL[:, :], T.b5[:, 0:8], rel, op.add, "b5", "HL", float(TOP), op.min)
+        step("H", False, None if k else guest_points)
+        guests(k)
+        if k == 0:
+            ts(T.M48[:, :], T.G48[:, :], pg, op.is_equal, "G48 CF", "M48")
+            fill(T.M48[:, me::6], 0.0, "M48")
+            ts(T.N6F[:, 0:3], T.N6[:, 0:3], -6.0, op.mult, "N6", "N6F")
+            tt(T.NM[:, 0:3], T.NI[:, 0:3], T.N6F[:, 0:3], op.add, "NI N6F", "NM")
+            ts(T.NG[:, 0:3], T.NM[:, 0:3], float(me), op.is_gt, "NM", "NG")
+            tt(T.NK[:, 0:3], T.NM[:, 0:3], T.NG[:, 0:3], op.subtract, "NM NG", "NK")
+            ts(T.LR[:, 0:3], T.NK[:, 0:3], 4.0, op.min, "NK", "LR")
+        step("H", False)
+        step("H", True)
+        replies(k)
+        if k < R - 1:
+            dispatch(k + 1)
+
+    to_list()
+    cp(T.YS[:, :], T.b5[:, 0:8], "b5", "YS")
+    dma("y", "sty", T.y[:, :], T.YS[:, :], "YS")
+
+    g.wait_ge(T.sem.sty, 16)
+    g.wait_ge(T.sem.sent, sent[0])
+    for q in "vtsc":
+        if known["c"].get(q, 0) < count[q]:
+            g.wait_ge(T.sem[q], count[q])

@@ -7,6 +7,8 @@ TOP = TT + OFF
 W = TOP + 8
 BIG = 8388608.0
 HOLD = 32768.0
+PRE = (10, 14)
+MIX = ((0, 1, 0, 0, 0, 0, 0, 0, 0, 0), (0, 1, 1, 1, 0, 1, 1, 0, 1, 0), (0, 2, 0, 0, 0, 0, 0, 0, 0, 0))
 
 
 def _s(n, dtype="float32"):
@@ -50,11 +52,11 @@ def slot(owner, other):
 def engine_split(topo, src, dsts):
     on = [d for d in dsts if topo.chip(d) == topo.chip(src)]
     off = [d for d in dsts if topo.chip(d) != topo.chip(src)]
-    eo = topo.engines(src, off[0]) if off else []
+    eo = topo.engines(src, off[0])
     out = {}
-    for ds, es in ((off, eo), (on, [e for e in topo.engines(src, on[0]) if e not in eo] if on else [])):
+    for ds, es in ((off, eo), (on, [e for e in topo.engines(src, on[0]) if e not in eo])):
         per = 1
-        while ds and 2 * per * len(ds) <= len(es):
+        while 2 * per * len(ds) <= len(es):
             per *= 2
         for i, d in enumerate(ds):
             out[d] = es[i * per:(i + 1) * per]
@@ -234,13 +236,13 @@ def rank_program(g, core, T, topo):
     def dispatch(k, extra=None):
         ms = "MS%d" % k
         ts(T.QI[:, :], T.US[:, :], 1.0 / TT, op.mult, "US", "QI", -0.4995, op.add)
+        tt(T.VV[:, :], T.US[:, :].indirect(T.L6[:, 0:3]), T.CV[:, :], op.add, "US L6 CV", "VV")
         tt(T.OH[:, :], T.QI[:, :].indirect(T.L6[:, 0:3]), T.QC[:, :], op.is_equal, "QI L6 QC", "OH")
         mm(T.b7[:, 0:48], T.UT[:, :], T.OH[:, :], True, True, "UT OH", "b7")
-        tt(T.VV[:, :], T.US[:, :].indirect(T.L6[:, 0:3]), T.CV[:, :], op.add, "US L6 CV", "VV")
+        tt(T.BT[:, 1::2], T.CJ[:, :], T.OH[:, :], op.mult, "CJ OH", "BTj")
         if extra:
             extra()
         scan(T.SS[:, :], T.R6[:, :], T.b7[:, 0:48], op.mult, op.max, "R6 b7", "SS")
-        tt(T.BT[:, 1::2], T.CJ[:, :], T.OH[:, :], op.mult, "CJ OH", "BTj")
         tt(T.BT[:, 0::2], T.VV[:, :], T.OH[:, :], op.mult, "VV OH", "BTt")
         tt(T.AA[:, :], T.SS[:, :].indirect(T.LA[:, 0:8]), T.IA[:, :], op.is_equal, "SS LA IA", "AA")
         for a in range(4):
@@ -252,13 +254,14 @@ def rank_program(g, core, T, topo):
         event("rq%d" % k, into, "LM%d" % k)
 
     def hold():
-        mm(T.b6[:, 0:128], T.AA[:, :], T.IDH[:, :], True, True, "AA IDH", "b6")
         ts(T.CHB[:, :], T.OH[:, :], HOLD, op.mult, "OH", "CHB", -HOLD, op.add)
+
+    def hold_own():
         ts(T.CHB[:, me::6], T.OH[:, me::6], HOLD, op.mult, "OH CHB", "CHB", -HOLD - rel, op.add)
-        ts(T.HCP[:, 0::5], T.US[:, 5::6], rel, op.add, "US", "HCP")
+        mm(T.b6[:, 0:128], T.AA[:, :], T.IDH[:, :], True, True, "AA IDH", "b6")
         do("s", lambda e: e.activation(T.AT[:, :], T.b6[:, 0:128], act.Copy), "b6", "AT")
 
-    def step(h, last, between=None):
+    def step(h, last):
         n, lst, pt, bk, bn, bc = (128, T.HL[:, 0:8], "PTH", "b3", "b4", "b5") if h == "H" else (80, T.GL[:, 0:5], "GT", "b0", "b1", "b2")
         ln, m = h + "L", n // 16
         X = lambda a: T[h + a]
@@ -266,27 +269,52 @@ def rank_program(g, core, T, topo):
         mm(T[bn][0:n, 0:40], T.ID[0:n, 0:n], X("CP")[0:n, :], True, False, "ID " + h + "CP", bn)
         tt(X("P")[:, :], T.PW[:, :].indirect(lst), T[pt][:, 0:n], op.mult, "PWa PWb " + ln + " " + pt, h + "P")
         mm(T[bk][0:n, 0:40], X("P")[:, :], T.RK[:, :], False, True, h + "P RK", bk)
+        yield
         cp(X("N")[:, :], T.NW[:, :].indirect(lst), "NWc NWv NWa " + ln, h + "N")
         mm(T[bn][0:n, 0:40], X("N")[:, :], T.RN[:, :], False, True, h + "N RN", bn)
-        if between:
-            between()
+        yield
         scan(X("PM")[0:n, :], T.R5[0:n, :], T[bk][0:n, 0:40], op.max, op.min, "R5 " + bk, h + "PM")
+        yield
         tt(X("E")[0:n, :], X("PM")[0:n, :], T[bk][0:n, 0:40], op.is_equal, h + "PM " + bk, h + "E")
+        yield
         tt(X("NE")[0:n, :], X("PM")[0:n, :], T[bk][0:n, 0:40], op.not_equal, h + "PM " + bk, h + "NE")
+        yield
         tt(X("D1")[0:n, :], X("E")[0:n, :], T[bn][0:n, 0:40], op.mult, h + "E " + bn, h + "D1")
+        yield
         scan(X("Z")[0:n, :], X("NE")[0:n, :], X("D1")[0:n, :], op.mult, op.add, h + "NE " + h + "D1", h + "Z")
+        yield
         if not last:
             tt(X("D")[:, :], X("Z")[:, :].indirect(T.LD[:, 0:8]), T.MI[:, :], op.mult, h + "Z LD MI", h + "D")
             mm(T[bc][:, 0:m], X("D")[0:n, :], T.GSH[0:n, 0:m], True, True, h + "D GSH", bc)
+            yield
             cp(X("CP")[0:n, 0::5], X("Z")[0:n, 4::5], h + "Z", h + "CP")
+            yield
             ts(lst, T[bc][:, 0:m], float(TOP), op.min, bc, ln)
+            yield
         elif h == "H":
             tt(T.CHB[:, me::6], T.CHB[:, me::6], T.HZ[:, 4::5], op.add, "CHB HZ", "CHB")
+            yield
         else:
             tt(T.GDF[:, :], T.GZ[:, :].indirect(T.LD[:, 0:8]), T.MI[:, :], op.mult, "GZ LD MI", "GDF")
             mm(T[bc][:, 0:m], T.GDF[0:n, :], T.GS[0:n, 0:m], True, True, "GDF GS", bc)
+            yield
 
-    def guests(k):
+    def home(k):
+        if k:
+            to_list()
+            ts(T.HCP[:, 0::5], T.US[:, 5::6], rel, op.add, "US", "HCP")
+            yield
+            hold()
+            yield
+            ts(T.HL[:, :], T.b5[:, 0:8], rel, op.add, "b5", "HL", float(TOP), op.min)
+            yield
+            hold_own()
+            yield
+        for i in range(S):
+            for _ in step("H", i == S - 1):
+                yield
+
+    def guests(k, own):
         lm = "LM%d" % k
         cp(T.JL[:, 0:5], T[lm][:, 1::2], lm, "JL")
         do("s", lambda e: e.activation(T.GT[:, :], T.PT[:, :].indirect(T.JL[:, 0:5]), act.Copy), "PT0 PT1 PT2 PT3 JL", "GT")
@@ -296,7 +324,11 @@ def rank_program(g, core, T, topo):
         mm(T.b2[0:80, 0:8], T.EX[:, :], T.GSH[:, :], True, True, "EX GSH", "b2")
         cp(T.GCP[0:80, 0::5], T.b2[0:80, 0:8], "b2", "GCP")
         for i in range(S):
-            step("G", i == S - 1)
+            mine = step("G", i == S - 1)
+            for pieces in MIX[i]:
+                next(mine, None)
+                for _ in range(pieces):
+                    next(own, None)
         ts(T["RT%d" % k][:, 0:5], T.b2[:, 0:5], -rel, op.add, "b2", "RT%d" % k)
         send(lambda q: T["RT%d" % k][:, slot(me, q):slot(me, q) + 1], lambda q: T["RL%d" % k][:, slot(q, me):slot(q, me) + 1], "rt%d" % k, "RT%d" % k)
         event("rt%d" % k, into, "RL%d" % k)
@@ -342,18 +374,20 @@ def rank_program(g, core, T, topo):
     ts(T.LD[:, :], T.IC[:, 0:8], 5.0, op.mult, "IC", "LD", 4.0, op.add)
     ts(T.HL[:, :], T.T0I[:, :], rel, op.add, "T0I", "HL", float(TOP), op.min)
     hold()
+    ts(T.HCP[:, 0::5], T.US[:, 5::6], rel, op.add, "US", "HCP")
+    hold_own()
     ts(T.RK[:, :], T.RKI[:, :], p2, op.is_equal, "RKI CF", "RK")
     fill(T.RK[:, 0::5], 0.0, "RK")
     ts(T.RN[:, :], T.RNI[:, :], p, op.is_equal, "RNI CF", "RN")
     fill(T.RN[:, 0::5], 0.0, "RN")
 
     for k in range(R):
-        if k:
-            hold()
-            to_list()
-            ts(T.HL[:, :], T.b5[:, 0:8], rel, op.add, "b5", "HL", float(TOP), op.min)
-        step("H", False, None if k else guest_points)
-        guests(k)
+        own = home(k)
+        for i in range(PRE[min(k, 1)]):
+            next(own, None)
+            if i == 1 and k == 0:
+                guest_points()
+        guests(k, own)
         if k == 0:
             ts(T.M48[:, :], T.G48[:, :], pg, op.is_equal, "G48 CF", "M48")
             fill(T.M48[:, me::6], 0.0, "M48")
@@ -362,8 +396,8 @@ def rank_program(g, core, T, topo):
             ts(T.NG[:, 0:3], T.NM[:, 0:3], float(me), op.is_gt, "NM", "NG")
             tt(T.NK[:, 0:3], T.NM[:, 0:3], T.NG[:, 0:3], op.subtract, "NM NG", "NK")
             ts(T.LR[:, 0:3], T.NK[:, 0:3], 4.0, op.min, "NK", "LR")
-        step("H", False)
-        step("H", True)
+        for _ in own:
+            pass
         replies(k)
         if k < R - 1:
             dispatch(k + 1)

@@ -5,10 +5,11 @@ N, TT, P, R, S = 6, 1024, 128, 3, 3
 OFF = 8
 TOP = TT + OFF
 W = TOP + 8
-BIG = 8388608.0
+KEY = 16384.0
+BIG = 2.0 ** 37
 HOLD = 32768.0
-PRE = (10, 14)
-MIX = ((0, 1, 0, 0, 0, 0, 0, 0, 0, 0), (0, 1, 1, 1, 0, 1, 1, 0, 1, 0), (0, 2, 0, 0, 0, 0, 0, 0, 0, 0))
+PRE = (5, 6)
+MIX = ((1, 2, 0, 0, 1, 2, 1, 1, 0), (0, 2, 0, 0, 1, 1, 0, 1, 0), (0, 1, 0, 0, 0, 0, 1, 1, 0))
 
 
 def _s(n, dtype="float32"):
@@ -21,7 +22,7 @@ SCRATCH = {
     "CI": _s(8, "int32"), "CF": _s(8), "CX": _s(4), "IC": _s(128, "int32"), "ICM": _s(128, "int32"),
     "MI": _s(128), "IA": _s(128), "ID": _s(128), "IDH": _s(128, "float16"), "UA": _s(128), "UB": _s(128), "UT": _s(128, "bfloat16"),
     "GS": _s(8), "GSH": _s(8, "float16"), "M48": _s(48), "G48": _s(48), "QC": _s(48), "CV": _s(48), "CJ": _s(48), "CJ0": _s(48),
-    "RKI": _s(40), "RNI": _s(40), "RK": _s(40), "RN": _s(40), "CR": _s(40, "bfloat16"), "ON": _s(128, "bfloat16"), "R5": _s(40), "R6": _s(48),
+    "RKI": _s(40), "RNI": _s(40), "RK": _s(80), "RN": _s(40), "CR": _s(80, "bfloat16"), "ON": _s(128, "bfloat16"), "R5": _s(80), "R6": _s(48),
     "SV": _s(128), "SEL": _s(128, "float16"), "NI": _s(4), "N6": _s(4, "int32"), "N6F": _s(4), "NM": _s(4), "NG": _s(4), "NK": _s(4),
     "L6": _s(4, "uint16"), "LR": _s(4, "uint16"), "LA": _s(8, "uint16"), "LD": _s(8, "uint16"), "LT": _s(8, "uint16"),
     "HL": _s(8, "uint16"), "GL": _s(8, "uint16"), "JL": _s(8, "uint16"),
@@ -31,7 +32,7 @@ SCRATCH = {
 }
 for _t in "HG":
     _n = 128 if _t == "H" else 80
-    SCRATCH.update({_t + "P": _s(_n), _t + "N": _s(_n), _t + "PM": _s(40), _t + "E": _s(40), _t + "NE": _s(40), _t + "D1": _s(40),
+    SCRATCH.update({_t + "P": _s(_n), _t + "N": _s(_n), _t + "SC": _s(80), _t + "D0": _s(40), _t + "D1": _s(40),
                     _t + "Z": _s(40), _t + "D": _s(128, "float16"), _t + "CP": _s(40)})
 for _k in range(R):
     SCRATCH["MS%d" % _k] = _s(12, "float16")
@@ -190,8 +191,10 @@ def rank_program(g, core, T, topo):
     fill(T.US[:, :], 0.0, "US")
     fill(T.R6[:, :], 1.0, "R6")
     fill(T.R6[:, 0::6], 0.0, "R6")
-    for ap, n, x, w in ((T.HCP[:, :], 40, rel, "HCP"), (T.GCP[:, :], 40, rel, "GCP"), (T.GZ[:, :], 40, 0.0, "GZ"), (T.R5[:, :], 40, -BIG, "R5"),
-                        (T.R5[:, 0::5], 8, BIG, "R5"), (T.CR[:, :], 40, 0.0, "CR"), (T.CR[:, 0::5], 8, -0.5, "CR")):
+    for ap, n, x, w in ((T.HCP[:, :], 40, rel, "HCP"), (T.GCP[:, :], 40, rel, "GCP"), (T.GZ[:, :], 40, 0.0, "GZ"), (T.R5[:, 0::2], 40, 2 * BIG, "R5"),
+                        (T.R5[:, 1::2], 40, KEY / 2, "R5"), (T.R5[:, 0::10], 8, -BIG, "R5"), (T.R5[:, 1::10], 8, -BIG - KEY, "R5"),
+                        (T.CR[:, 0::2], 40, KEY / 2, "CR"), (T.CR[:, 1::2], 40, -KEY / 2, "CR"), (T.CR[:, 0::10], 8, 2 * BIG, "CR"),
+                        (T.CR[:, 1::10], 8, BIG, "CR")):
         sfill(ap, n, x, w)
     rs, an = op.arith_shift_right, op.bitwise_and
     ts(T.CI[:, 1:2], T.CI[:, 0:1], 15, an, "CI0", "CI1")
@@ -265,23 +268,21 @@ def rank_program(g, core, T, topo):
         n, lst, pt, bk, bn, bc = (128, T.HL[:, 0:8], "PTH", "b3", "b4", "b5") if h == "H" else (80, T.GL[:, 0:5], "GT", "b0", "b1", "b2")
         ln, m = h + "L", n // 16
         X = lambda a: T[h + a]
-        mm(T[bk][0:n, 0:40], T.ON[0:1, 0:n], T.CR[0:1, :], True, False, "ON CR", bk)
+        mm(T[bk][0:n, 0:80], T.ON[0:1, 0:n], T.CR[0:1, :], True, False, "ON CR", bk)
         mm(T[bn][0:n, 0:40], T.ID[0:n, 0:n], X("CP")[0:n, :], True, False, "ID " + h + "CP", bn)
         tt(X("P")[:, :], T.PW[:, :].indirect(lst), T[pt][:, 0:n], op.mult, "PWa PWb " + ln + " " + pt, h + "P")
-        mm(T[bk][0:n, 0:40], X("P")[:, :], T.RK[:, :], False, True, h + "P RK", bk)
+        mm(T[bk][0:n, 0:80], X("P")[:, :], T.RK[:, :], False, True, h + "P RKa RKb", bk)
         yield
         cp(X("N")[:, :], T.NW[:, :].indirect(lst), "NWc NWv NWa " + ln, h + "N")
         mm(T[bn][0:n, 0:40], X("N")[:, :], T.RN[:, :], False, True, h + "N RN", bn)
         yield
-        scan(X("PM")[0:n, :], T.R5[0:n, :], T[bk][0:n, 0:40], op.max, op.min, "R5 " + bk, h + "PM")
+        scan(X("SC")[0:n, :], T.R5[0:n, :], T[bk][0:n, 0:80], op.min, op.add, "R5 " + bk, h + "SC")
         yield
-        tt(X("E")[0:n, :], X("PM")[0:n, :], T[bk][0:n, 0:40], op.is_equal, h + "PM " + bk, h + "E")
+        tt(X("D1")[0:n, :], X("SC")[0:n, 0::2], T[bn][0:n, 0:40], op.min, h + "SC " + bn, h + "D1")
         yield
-        tt(X("NE")[0:n, :], X("PM")[0:n, :], T[bk][0:n, 0:40], op.not_equal, h + "PM " + bk, h + "NE")
+        ts(X("D0")[0:n, :], X("SC")[0:n, 0::2], 0.0, op.is_ge, h + "SC", h + "D0", -HOLD, op.mult)
         yield
-        tt(X("D1")[0:n, :], X("E")[0:n, :], T[bn][0:n, 0:40], op.mult, h + "E " + bn, h + "D1")
-        yield
-        scan(X("Z")[0:n, :], X("NE")[0:n, :], X("D1")[0:n, :], op.mult, op.add, h + "NE " + h + "D1", h + "Z")
+        scan(X("Z")[0:n, :], X("D0")[0:n, :], X("D1")[0:n, :], op.add, op.max, h + "D0 " + h + "D1", h + "Z")
         yield
         if not last:
             tt(X("D")[:, :], X("Z")[:, :].indirect(T.LD[:, 0:8]), T.MI[:, :], op.mult, h + "Z LD MI", h + "D")
@@ -376,8 +377,10 @@ def rank_program(g, core, T, topo):
     hold()
     ts(T.HCP[:, 0::5], T.US[:, 5::6], rel, op.add, "US", "HCP")
     hold_own()
-    ts(T.RK[:, :], T.RKI[:, :], p2, op.is_equal, "RKI CF", "RK")
-    fill(T.RK[:, 0::5], 0.0, "RK")
+    ts(T.RK[:, 0::2], T.RKI[:, :], p2, op.is_equal, "RKI CF", "RKa", -KEY, op.mult)
+    ts(T.RK[:, 1::2], T.RKI[:, :], p2, op.is_equal, "RKI CF", "RKb", KEY, op.mult)
+    fill(T.RK[:, 0::10], 0.0, "RKa")
+    fill(T.RK[:, 1::10], 0.0, "RKb")
     ts(T.RN[:, :], T.RNI[:, :], p, op.is_equal, "RNI CF", "RN")
     fill(T.RN[:, 0::5], 0.0, "RN")
 

@@ -2,14 +2,19 @@ from concourse.bass import DstId, RemoteDMATransfer
 from concourse.mybir import AluOpType, ActivationFunctionType
 
 N, TT, P, R, S = 6, 1024, 128, 3, 3
-OFF = 8
+OFF = 64
 TOP = TT + OFF
 W = TOP + 8
+FAR = 2048
 KEY = 16384.0
 BIG = 2.0 ** 37
 HOLD = 32768.0
-PRE = (5, 6)
-MIX = ((1, 2, 0, 0, 1, 2, 1, 1, 0), (0, 2, 0, 0, 1, 1, 0, 1, 0), (0, 1, 0, 0, 0, 0, 1, 1, 0))
+QB = 129
+BASE = QB - 1023.0 / 2048
+PRE = (2, 3)
+MIX = (((2, 1, 0, 0, 2, 0), (2, 1, 1, 0, 2, 0), (2, 1, 4, 7, 5)), ((0, 0, 1, 1, 1, 0), (2, 0, 0, 0, 2, 0), (2, 0, 1, 0, 1)))
+GAP0 = (9, 3)
+GAP = ((4, 6, 8, 3), (0, 0, 1, 1))
 
 
 def _s(n, dtype="float32"):
@@ -17,23 +22,28 @@ def _s(n, dtype="float32"):
 
 
 SCRATCH = {
-    "PW": _s(W, "int32"), "NW": _s(W, "int32"), "T0I": _s(8, "int32"),
+    "PW": _s(W, "int32"), "NW": _s(W, "bfloat16"), "T0I": _s(8, "int32"),
+    "NT": _s(40, "int32"), "NA": _s(40, "int32"), "NU": _s(40), "NP": _s(80, "int32"), "NS": _s(120, "bfloat16"),
+    "ND": ("dram", [16, TT], "bfloat16"),
     "P4": _s(32, "int32"), "P4H": _s(32, "float16"), "PD": _s(160, "float16"), "PT": _s(640), "PTH": _s(128),
-    "CI": _s(8, "int32"), "CF": _s(8), "CX": _s(4), "IC": _s(128, "int32"), "ICM": _s(128, "int32"),
-    "MI": _s(128), "IA": _s(128), "ID": _s(128), "IDH": _s(128, "float16"), "UA": _s(128), "UB": _s(128), "UT": _s(128, "bfloat16"),
-    "GS": _s(8), "GSH": _s(8, "float16"), "M48": _s(48), "G48": _s(48), "QC": _s(48), "CV": _s(48), "CJ": _s(48), "CJ0": _s(48),
-    "RKI": _s(40), "RNI": _s(40), "RK": _s(80), "RN": _s(40), "CR": _s(80, "bfloat16"), "ON": _s(128, "bfloat16"), "R5": _s(80), "R6": _s(48),
-    "SV": _s(128), "SEL": _s(128, "float16"), "NI": _s(4), "N6": _s(4, "int32"), "N6F": _s(4), "NM": _s(4), "NG": _s(4), "NK": _s(4),
+    "CI": _s(8, "int32"), "CF": _s(8), "C5": _s(3), "CX": _s(4), "IC": _s(128, "int32"), "ICM": _s(128, "int32"),
+    "MI": _s(128), "IA": _s(128), "IDS": _s(128), "IDH": _s(128, "float16"), "UT": _s(128, "bfloat16"),
+    "GS": _s(8), "GSL": _s(8), "GSH": _s(8, "float16"), "M48": _s(48), "G48": _s(48), "QC": _s(48), "CV": _s(48), "CJ": _s(48), "CJ0": _s(48),
+    "RKI": _s(40), "RNI": _s(40), "RK": _s(80), "RN0": _s(40, "bfloat16"), "RN1": _s(40, "bfloat16"), "RN2": _s(40, "bfloat16"),
+    "RNA": _s(40, "bfloat16"), "RNB": _s(40, "bfloat16"),
+    "CR": _s(80, "bfloat16"), "ON": _s(128, "bfloat16"), "R5": _s(80), "R6": _s(48),
+    "SA": _s(128, "int32"), "SB": _s(128, "int32"), "SV": _s(128), "SEL": _s(128, "float16"),
+    "NI": _s(4), "N6": _s(4, "int32"), "N6F": _s(4), "NM": _s(4), "NG": _s(4), "NK": _s(4),
     "L6": _s(4, "uint16"), "LR": _s(4, "uint16"), "LA": _s(8, "uint16"), "LD": _s(8, "uint16"), "LT": _s(8, "uint16"),
     "HL": _s(8, "uint16"), "GL": _s(8, "uint16"), "JL": _s(8, "uint16"),
-    "US": _s(48), "QI": _s(48, "int32"), "OH": _s(48, "bfloat16"), "VV": _s(48), "BT": _s(96, "float16"), "SS": _s(48),
-    "AA": _s(128, "float16"), "AT": _s(128), "T1": _s(12), "T2": _s(12), "CHB": _s(48), "RX": _s(48), "DX": _s(128), "YS": _s(8),
-    "GT": _s(80), "LF": _s(8), "EX": _s(80, "float16"), "GDF": _s(128),
+    "US": _s(48), "QI": _s(48, "bfloat16"), "OH": _s(48, "bfloat16"), "VV": _s(48), "BT": _s(96, "float16"), "SS": _s(48),
+    "AA": _s(128, "float16"), "AT": _s(128), "M12": _s(12), "MK": _s(24), "TM": _s(24), "CHB": _s(48), "RX": _s(48), "DX": _s(128), "YS": _s(8),
+    "GT": _s(80), "GDF": _s(128),
 }
 for _t in "HG":
     _n = 128 if _t == "H" else 80
-    SCRATCH.update({_t + "P": _s(_n), _t + "N": _s(_n), _t + "SC": _s(80), _t + "D0": _s(40), _t + "D1": _s(40),
-                    _t + "Z": _s(40), _t + "D": _s(128, "float16"), _t + "CP": _s(40)})
+    SCRATCH.update({_t + "P": _s(_n), _t + "N": _s(_n, "bfloat16"), _t + "SC": _s(80), _t + "D0": _s(40), _t + "D1": _s(40),
+                    _t + "Z": _s(40), _t + "D": _s(128, "float16"), _t + "V0": _s(40 if _t == "G" else 8), _t + "V1": _s(40 if _t == "G" else 8)})
 for _k in range(R):
     SCRATCH["MS%d" % _k] = _s(12, "float16")
     SCRATCH["LM%d" % _k] = _s(10, "float16")
@@ -42,7 +52,7 @@ for _k in range(R):
 for _k in range(8):
     SCRATCH["b%d" % _k] = ("psum", [128, 512], "float32")
 
-SEMAPHORES = ["v", "t", "s", "c", "ltet", "lpts", "lpl", "lnb", "sty", "pd", "sent"] + ["rq%d" % k for k in range(R)] + ["rt%d" % k for k in range(R)]
+SEMAPHORES = ["v", "t", "s", "c", "ltet", "lpts", "lpl", "lnt", "lnd", "lnb", "sty", "pd", "sent"] + ["rq%d" % k for k in range(R)] + ["rt%d" % k for k in range(R)]
 BANKS = ["b%d" % k for k in range(8)]
 
 
@@ -143,8 +153,11 @@ def rank_program(g, core, T, topo):
     def fill(ap, x, w):
         do("v", lambda e: e.memset(ap, x), "", w)
 
+    def sc(out, a, r, w, bias=0.0, scale=1.0, f=act.Copy):
+        do("s", lambda e: e.activation(out, a, f, bias=bias, scale=scale), r, w)
+
     def sfill(ap, n, x, w):
-        do("s", lambda e: e.activation(ap, T.R6[:, 0:n], act.Copy, bias=x, scale=0.0), "R6", w)
+        sc(ap, T.R6[:, 0:n], "R6", w, bias=x, scale=0.0)
 
     def scan(out, d0, d1, o0, o1, r, w):
         do("v", lambda e: e.tensor_tensor_scan(out, d0, d1, 0.0, o0, o1), r, w)
@@ -174,24 +187,28 @@ def rank_program(g, core, T, topo):
 
     fill(T.P4[:, :], 0, "P4")
     dma("y", "ltet", T.T0I[:, :], T.tet0[:, :])
+    dma("s", "lnt", T.NT[:, 0:32], T.nbr[:, :])
     for b in range(4):
         dma("y" if b % 2 else "s", "lpts", T.P4[32 * b:32 * b + 24, :], T.pts[:, 32 * b:32 * b + 32], "", "P4")
     for k in range(8):
-        dma("y" if k % 2 else "s", "lpl", T.PW[16 * k:16 * k + 16, OFF:OFF + TT], T.planes[:, :])
+        dma("y" if k % 2 else "s", "lpl", T.PW[16 * k:16 * k + 16, OFF:TOP], T.planes[:, :])
 
+    fill(T.R6[:, :], 1.0, "R6")
+    fill(T.ON[:, :], 1.0, "ON")
     iota(T.CI[:, 0:1], [[0, 1]], 0, 1, "CI0", small=False)
     iota(T.IC[:, :], [[1, 128]], 0, 0, "IC", small=False)
-    iota(T.QC[:, :], [[0, 8], [1, 6]], 0, 0, "QC")
-    iota(T.SV[:, :], [[3, 8], [0, 4], [1, 4]], 0, 0, "SV")
-    iota(T.NW[:, 0:W // 2], [[1, W // 2]], 0, 0, "NWc", small=False)
+    iota(T.NT[:, 32:40], [[1, 8]], TT * me, 8, "NT1", small=False)
+    iota(T.QC[:, :], [[0, 8], [1, 6]], QB, 0, "QC")
+    do("c", lambda e: e.affine_select(T.UT[:, :], T.ON[:, :], [[1, 128]], op.is_gt, 0.0, 0, -1), "ON", "UT")
+    do("c", lambda e: e.affine_select(T.UT[:, :], T.UT[:, :], [[1, 128]], op.not_equal, 256.0, 0, -1), "UT", "UT")
+    iota(T.RKI[:, :], [[4, 8], [-1, 5]], 4, 0, "RKI")
     event("ltet", 16, "T0I")
+    event("lnt", 16, "NT0")
     event("lpts", 64, "P4")
     event("lpl", 128, "PWa")
 
-    fill(T.US[:, :], 0.0, "US")
-    fill(T.R6[:, :], 1.0, "R6")
     fill(T.R6[:, 0::6], 0.0, "R6")
-    for ap, n, x, w in ((T.HCP[:, :], 40, rel, "HCP"), (T.GCP[:, :], 40, rel, "GCP"), (T.GZ[:, :], 40, 0.0, "GZ"), (T.R5[:, 0::2], 40, 2 * BIG, "R5"),
+    for ap, n, x, w in ((T.GZ[:, :], 40, 0.0, "GZ"), (T.GV0[:, :], 40, 0.0, "GV0"), (T.GV1[:, :], 40, 0.0, "GV1"), (T.R5[:, 0::2], 40, 2 * BIG, "R5"),
                         (T.R5[:, 1::2], 40, KEY / 2, "R5"), (T.R5[:, 0::10], 8, -BIG, "R5"), (T.R5[:, 1::10], 8, -BIG - KEY, "R5"),
                         (T.CR[:, 0::2], 40, KEY / 2, "CR"), (T.CR[:, 1::2], 40, -KEY / 2, "CR"), (T.CR[:, 0::10], 8, 2 * BIG, "CR"),
                         (T.CR[:, 1::10], 8, BIG, "CR")):
@@ -211,84 +228,206 @@ def rank_program(g, core, T, topo):
     ts(T.MI[:, :], T.ICM[:, :], p15, op.is_equal, "ICM CF", "MI")
     ts(T.GS[:, :], T.IC[:, 0:8], pg, op.is_equal, "IC CF", "GS")
     ts(T.NI[:, 0:3], T.IC[:, 0:3], 16.0, op.mult, "IC CF", "NI", p15, op.add)
-    ts(T.UB[:, :], T.IC[:, :], p, op.is_equal, "IC CF", "UB", 256.0, op.mult)
     ts(T.N6[:, 0:3], T.NI[:, 0:3], 1.0 / 6, op.mult, "NI", "N6", -2.5 / 6, op.add)
-    ts(T.UA[:, :], T.IC[:, :], p, op.is_gt, "IC CF", "UA")
     ts(T.L6[:, 0:3], T.N6[:, 0:3], 6.0, op.mult, "N6", "L6", 5.0, op.add)
-    tt(T.UT[:, :], T.UA[:, :], T.UB[:, :], op.add, "UA UB", "UT")
-    fill(T.NW[:, W // 2:W], 0, "NWv")
 
     cp(T.P4H[:, :], T.P4[:, :], "P4", "P4H")
     send(lambda q: T.P4H[:, :], lambda q: T.PD[:, 32 * slot(q, me):32 * slot(q, me) + 32], "pd", "P4H")
     event("pd", into, "PD")
+    iota(T.RNI[:, :], [[16, 8], [-1, 5]], 4, 0, "RNI")
+    iota(T.C5[:, :], [[-5, 3]], 0, 1, "C5")
+    iota(T.G48[:, :], [[1, 8], [0, 6]], 0, 0, "G48")
 
-    for k in range(8):
-        dma("y", "lnb", T.NW[16 * k:16 * k + 4, OFF:OFF + TT], T.nbr[:, :], "", "NWc NWv")
-    event("lnb", 128, "NWa")
+    def spread(bank, at, n, src, b):
+        mm(T[bank][:, at:at + n], T.SEL[32 * b:32 * b + 32, :], T[src][32 * b:32 * b + 32, :], True, True, src + " SEL", bank)
 
-    tt(T.DX[:, :], T.T0I[:, :].indirect(T.LT[:, 0:8]), T.MI[:, :], op.mult, "T0I LT MI", "DX")
-    mm(T.b7[:, 0:8], T.DX[:, :], T.GS[:, :], True, True, "DX GS", "b7")
-    ts(T.CV[:, :], T.QC[:, :], float(-TT), op.mult, "QC", "CV", float(OFF), op.add)
-    ts(T.CX[:, 0:1], p5, 160.0, op.mult, "CF", "CX0", p31, op.add)
-    ts(T.CJ0[:, :], T.QC[:, :], float(me), op.is_lt, "QC", "CJ0", -32.0, op.mult)
-    ts(T.CX[:, 1:2], podd, -1.0, op.mult, "CF", "CX1", 1.0, op.add)
-    cp(T.US[:, 5::6], T.b7[:, 0:8], "b7", "US")
-    ts(T.LA[:, :], T.IC[:, 0:8], 6.0, op.mult, "IC", "LA", 5.0, op.add)
-    ts(T.CJ[:, :], T.CJ0[:, :], T.CX[:, 0:1], op.add, "CJ0 CX0", "CJ", 32.0 * me, op.add)
+    def guest_points():
+        for b, bank in enumerate(("b0", "b1", "b2", "b6")):
+            spread(bank, 0, 160, "PD", b)
+        for b, bank in ((0, "b0"), (2, "b2")):
+            sc(T.PT[:, 160 * b:160 * b + 160], T[bank][:, 0:160], bank + " CX2", "PT%d" % b, bias=T.CX[:, 2:3], f=act.Identity)
+        yield
+        for b, bank in ((1, "b1"), (3, "b6")):
+            ts(T.PT[:, 160 * b:160 * b + 160], T[bank][:, 0:160], T.CX[:, 2:3], op.add, bank + " CX2", "PT%d" % b)
+        yield
 
-    def dispatch(k, extra=None):
+    def window():
+        for b in (1, 2, 0):
+            r = "NS%d" % b
+            dma("y", "lnd", T.ND[5 * b:5 * b + 4, :], T.NS[:, 40 * b:40 * b + 32], r)
+            dma("s", "lnd", T.ND[5 * b + 4:5 * b + 5, :], T.NS[:, 40 * b + 32:40 * b + 40], r)
+        dma("y", "lnd", T.ND[15:16, :], T.NS[:, 112:120], "NS2")
+        event("lnd", 7 * 16, "ND")
+        for k in range(8):
+            dma("y", "lnb", T.NW[16 * k:16 * k + 16, OFF:TOP], T.ND[:, :], "ND")
+        event("lnb", 128, "NWa")
+
+    def constants():
+        fill(T.US[:, :], 0.0, "US")
+        yield
+        ts(T.NA[:, :], T.NT[:, :], 10, rs, "NT0 NT1", "NA")
+        yield
+        fill(T.QI[:, :], 0.0, "QI")
+        yield
+        ts(T.NP[:, 40:80], T.NT[:, :], 63, an, "NT0 NT1", "NP1")
+        yield
+        ts(T.NU[:, :], T.NA[:, :], float(me), op.is_equal, "NA", "NU", FAR - rel, op.mult)
+        yield
+        ts(T.NP[:, 0:40], T.NT[:, :], 8192 - 64, an, "NT0 NT1", "NP0")
+        yield
+        cp(T.NS[:, 40:80], T.NP[:, 40:80], "NP1", "NS1")
+        yield
+        ts(T.NS[:, 80:120], T.NU[:, :], float(-FAR), op.add, "NU", "NS2")
+        yield
+        ts(T.CV[:, :], T.QC[:, :], -1.0, op.mult, "QC", "CV", QB - BASE + OFF / float(TT), op.add)
+        yield
+        ts(T.CJ0[:, :], T.QC[:, :], float(QB + me), op.is_lt, "QC", "CJ0", -32.0, op.mult)
+        yield
+        tt(T.NS[:, 0:40], T.NP[:, 0:40], T.NS[:, 80:120], op.subtract, "NP0 NS2", "NS0")
+        window()
+        yield
+        ts(T.CX[:, 0:1], p5, 160.0, op.mult, "CF", "CX0", p31, op.add)
+        yield
+        ts(T.CJ[:, :], T.CJ0[:, :], T.CX[:, 0:1], op.add, "CJ0 CX0", "CJ", 32.0 * me, op.add)
+        yield
+        ts(T.LA[:, :], T.IC[:, 0:8], 6.0, op.mult, "IC", "LA", 5.0, op.add)
+        yield
+        ts(T.IA[:, :], T.ICM[:, :], 256.0, op.add, "ICM", "IA")
+        yield
+        ts(T.SA[:, :], T.IC[:, :], 4, rs, "IC", "SA")
+        yield
+        ts(T.SB[:, :], T.IC[:, :], 3, an, "IC", "SB")
+        yield
+        ts(T.SV[:, :], T.SA[:, :], 3.0, op.mult, "SA", "SV")
+        yield
+        ts(T.CX[:, 1:2], podd, -1.0, op.mult, "CF", "CX1", 1.0, op.add)
+        yield
+        tt(T.SV[:, :], T.SV[:, :], T.SB[:, :], op.add, "SV SB", "SV")
+        yield
+        fill(T.M12[:, 0::2], float(TT), "M12a")
+        yield
+        fill(T.M12[:, 1::2], 1.0, "M12b")
+        yield
+        fill(T.SV[:, 3::4], -1000.0, "SV")
+        yield
+        ts(T.MK[:, 0:12], T.M12[:, :], T.CX[:, 1:2], op.mult, "M12a M12b CX1", "MK0")
+        yield
+        ts(T.MK[:, 12:24], T.M12[:, :], podd, op.mult, "M12a M12b CF", "MK1")
+        yield
+        ts(T.SEL[:, :], T.SV[:, :], p31, op.is_equal, "SV CF", "SEL")
+        yield
+        ts(T.CX[:, 2:3], p3, 3.0, op.is_equal, "CF", "CX2")
+        for b in range(4):
+            if b:
+                wait("t", "t", count["t"])
+            spread("b3", 32 * b, 32, "P4H", b)
+        sc(T.PTH[:, :], T.b3[:, 0:128], "b3 CX2", "PTH", bias=T.CX[:, 2:3], f=act.Identity)
+        yield
+        ts(T.RK[:, 0::2], T.RKI[:, :], p2, op.is_equal, "RKI CF", "RKa", -KEY, op.mult)
+        yield
+        ts(T.RK[:, 1::2], T.RKI[:, :], p2, op.is_equal, "RKI CF", "RKb", KEY, op.mult)
+        yield
+        fill(T.RK[:, 0::10], 0.0, "RKa")
+        yield
+        fill(T.RK[:, 1::10], 0.0, "RKb")
+        yield
+        ts(T.HL[:, :], T.T0I[:, :], rel, op.add, "T0I", "HL", float(TOP), op.min)
+        yield
+        fill(T.PW[:, 0:OFF], 0, "PWb0")
+        yield
+        fill(T.PW[:, TOP:W], 0, "PWb1")
+        yield
+        fill(T.NW[:, 0:OFF], 0.0, "NWp0")
+        yield
+        fill(T.NW[:, TOP:W], 0.0, "NWp1")
+        yield
+        ts(T.IDS[:, :], T.IC[:, :], p, op.is_equal, "IC CF", "IDS", 1.0 / TT, op.mult)
+        yield
+        ts(T.RN0[:, :], T.RNI[:, :], T.C5[:, 0:1], op.is_equal, "RNI C5", "RN0")
+        yield
+        ts(T.RN1[:, :], T.RNI[:, :], T.C5[:, 1:2], op.is_equal, "RNI C5", "RN1")
+        yield
+        tt(T.RNA[:, :], T.RN0[:, :], T.RN1[:, :], op.add, "RN0 RN1", "RNA")
+        yield
+        ts(T.GSH[:, :], T.IC[:, 0:8], pg, op.is_equal, "IC CF", "GSH")
+        yield
+        ts(T.LD[:, :], T.IC[:, 0:8], 5.0, op.mult, "IC", "LD", 4.0, op.add)
+        yield
+
+    def dispatch(k, more):
         ms = "MS%d" % k
-        ts(T.QI[:, :], T.US[:, :], 1.0 / TT, op.mult, "US", "QI", -0.4995, op.add)
-        tt(T.VV[:, :], T.US[:, :].indirect(T.L6[:, 0:3]), T.CV[:, :], op.add, "US L6 CV", "VV")
+
+        def gap(i):
+            for _ in range(GAP[min(k, 1)][i]):
+                next(more, None)
+
         tt(T.OH[:, :], T.QI[:, :].indirect(T.L6[:, 0:3]), T.QC[:, :], op.is_equal, "QI L6 QC", "OH")
         mm(T.b7[:, 0:48], T.UT[:, :], T.OH[:, :], True, True, "UT OH", "b7")
+        if k:
+            scan(T.US[:, :], T.R6[:, :], T.b6[:, 128:176], op.mult, op.max, "R6 b6", "US")
+        gap(0)
         tt(T.BT[:, 1::2], T.CJ[:, :], T.OH[:, :], op.mult, "CJ OH", "BTj")
-        if extra:
-            extra()
+        tt(T.VV[:, :], T.US[:, :].indirect(T.L6[:, 0:3]), T.CV[:, :], op.add, "US L6 CV", "VV")
         scan(T.SS[:, :], T.R6[:, :], T.b7[:, 0:48], op.mult, op.max, "R6 b7", "SS")
+        gap(1)
         tt(T.BT[:, 0::2], T.VV[:, :], T.OH[:, :], op.mult, "VV OH", "BTt")
         tt(T.AA[:, :], T.SS[:, :].indirect(T.LA[:, 0:8]), T.IA[:, :], op.is_equal, "SS LA IA", "AA")
         for a in range(4):
             mm(T.b7[32 * a:32 * a + 32, 64:88], T.AA[:, 32 * a:32 * a + 32], T.BT[:, 24 * a:24 * a + 24], True, True, "AA BTj BTt", "b7")
-        ts(T.T1[:, :], T.b7[:, 64:76], T.CX[:, 1:2], op.mult, "b7 CX1", "T1")
-        ts(T.T2[:, :], T.b7[:, 76:88], podd, op.mult, "b7 CF", "T2")
-        tt(T[ms][:, :], T.T1[:, :], T.T2[:, :], op.add, "T1 T2", ms)
+        gap(2)
+        tt(T.TM[:, :], T.b7[:, 64:88], T.MK[:, :], op.mult, "b7 MK0 MK1", "TM")
+        gap(3)
+        tt(T[ms][:, :], T.TM[:, 0:12], T.TM[:, 12:24], op.add, "TM", ms)
         send(lambda q: T[ms][:, 2 * q:2 * q + 2], lambda q: T["LM%d" % k][:, 2 * slot(q, me):2 * slot(q, me) + 2], "rq%d" % k, ms)
         event("rq%d" % k, into, "LM%d" % k)
 
     def hold():
-        ts(T.CHB[:, :], T.OH[:, :], HOLD, op.mult, "OH", "CHB", -HOLD, op.add)
+        ts(T.CHB[:, :], T.OH[:, :], HOLD, op.mult, "OH", "CHB", TT * BASE - HOLD, op.add)
 
-    def hold_own():
-        ts(T.CHB[:, me::6], T.OH[:, me::6], HOLD, op.mult, "OH CHB", "CHB", -HOLD - rel, op.add)
+    def turn():
         mm(T.b6[:, 0:128], T.AA[:, :], T.IDH[:, :], True, True, "AA IDH", "b6")
-        do("s", lambda e: e.activation(T.AT[:, :], T.b6[:, 0:128], act.Copy), "b6", "AT")
+        sc(T.AT[:, :], T.b6[:, 0:128], "b6", "AT")
 
-    def step(h, last):
+    def step(h, i):
+        last = i == S - 1
         n, lst, pt, bk, bn, bc = (128, T.HL[:, 0:8], "PTH", "b3", "b4", "b5") if h == "H" else (80, T.GL[:, 0:5], "GT", "b0", "b1", "b2")
         ln, m = h + "L", n // 16
         X = lambda a: T[h + a]
-        mm(T[bk][0:n, 0:80], T.ON[0:1, 0:n], T.CR[0:1, :], True, False, "ON CR", bk)
-        mm(T[bn][0:n, 0:40], T.ID[0:n, 0:n], X("CP")[0:n, :], True, False, "ID " + h + "CP", bn)
-        tt(X("P")[:, :], T.PW[:, :].indirect(lst), T[pt][:, 0:n], op.mult, "PWa PWb " + ln + " " + pt, h + "P")
+        ones = lambda: mm(T[bk][0:n, 0:80], T.ON[0:1, 0:n], T.CR[0:1, :], True, False, "ON CR", bk)
+        left = lambda j: mm(T[bn][0:n, 0:40], T.IDS[0:n, 0:n], X("V%d" % j)[0:n, :], not j, False, "IDS " + h + "V%d" % j, bn)
+        if not i:
+            ones()
+        sc(X("N")[:, :], T.NW[:, :].indirect(lst), "NWp0 NWp1 NWa " + ln, h + "N")
+        tt(X("P")[:, :], T.PW[:, :].indirect(lst), T[pt][:, 0:n], op.mult, "PWa PWb0 PWb1 " + ln + " " + pt, h + "P")
         mm(T[bk][0:n, 0:80], X("P")[:, :], T.RK[:, :], False, True, h + "P RKa RKb", bk)
-        yield
-        cp(X("N")[:, :], T.NW[:, :].indirect(lst), "NWc NWv NWa " + ln, h + "N")
-        mm(T[bn][0:n, 0:40], X("N")[:, :], T.RN[:, :], False, True, h + "N RN", bn)
+        if last:
+            mm(T[bn][0:n, 0:40], X("N")[:, :], T.RNB[:, :], h == "H", True, h + "N RNB", bn)
+        else:
+            mm(T[bn][0:n, 0:40], X("N")[:, :], T.RNA[:, :], True, True, h + "N RNA", bn)
         yield
         scan(X("SC")[0:n, :], T.R5[0:n, :], T[bk][0:n, 0:80], op.min, op.add, "R5 " + bk, h + "SC")
+        if h == "G":
+            sc(X("D0")[0:n, :], X("SC")[0:n, 0::2], h + "SC", h + "D0", scale=-1.0)
+        if not last:
+            ones()
         yield
         tt(X("D1")[0:n, :], X("SC")[0:n, 0::2], T[bn][0:n, 0:40], op.min, h + "SC " + bn, h + "D1")
+        if h == "H":
+            ts(X("D0")[0:n, :], X("SC")[0:n, 0::2], -1.0, op.mult, h + "SC", h + "D0")
+        if h == "G" and i == S - 2:
+            left(0)
         yield
-        ts(X("D0")[0:n, :], X("SC")[0:n, 0::2], 0.0, op.is_ge, h + "SC", h + "D0", -HOLD, op.mult)
-        yield
-        scan(X("Z")[0:n, :], X("D0")[0:n, :], X("D1")[0:n, :], op.add, op.max, h + "D0 " + h + "D1", h + "Z")
+        if h == "H" and i:
+            tt(T.CHB[:, me::6], T.CHB[:, me::6], T["HV%d" % (i - 1)][:, :], op.add, "CHB HV%d" % (i - 1), "CHB")
+        scan(X("Z")[0:n, :], X("D0")[0:n, :], X("D1")[0:n, :], op.min, op.max, h + "D0 " + h + "D1", h + "Z")
         yield
         if not last:
+            v, c = (T["HV%d" % i][:, :], 1) if h == "H" else (T["GV%d" % i][0:n, 0::5], TT)
+            sc(v, X("Z")[0:n, 4::5], h + "Z", h + "V%d" % i, bias=float(-FAR * c), scale=float(c), f=act.Relu)
             tt(X("D")[:, :], X("Z")[:, :].indirect(T.LD[:, 0:8]), T.MI[:, :], op.mult, h + "Z LD MI", h + "D")
             mm(T[bc][:, 0:m], X("D")[0:n, :], T.GSH[0:n, 0:m], True, True, h + "D GSH", bc)
-            yield
-            cp(X("CP")[0:n, 0::5], X("Z")[0:n, 4::5], h + "Z", h + "CP")
+            if h == "G" and i == S - 2:
+                left(1)
             yield
             ts(lst, T[bc][:, 0:m], float(TOP), op.min, bc, ln)
             yield
@@ -303,110 +442,89 @@ def rank_program(g, core, T, topo):
     def home(k):
         if k:
             to_list()
-            ts(T.HCP[:, 0::5], T.US[:, 5::6], rel, op.add, "US", "HCP")
             yield
             hold()
+            turn()
             yield
-            ts(T.HL[:, :], T.b5[:, 0:8], rel, op.add, "b5", "HL", float(TOP), op.min)
-            yield
-            hold_own()
+            ts(T.HL[:, :], T.b5[:, 0:8], rel - TT * BASE, op.add, "b5", "HL", float(TOP), op.min)
             yield
         for i in range(S):
-            for _ in step("H", i == S - 1):
+            for _ in step("H", i):
                 yield
 
     def guests(k, own):
         lm = "LM%d" % k
         cp(T.JL[:, 0:5], T[lm][:, 1::2], lm, "JL")
-        do("s", lambda e: e.activation(T.GT[:, :], T.PT[:, :].indirect(T.JL[:, 0:5]), act.Copy), "PT0 PT1 PT2 PT3 JL", "GT")
-        cp(T.LF[:, 0:5], T[lm][:, 0::2], lm, "LF")
-        ts(T.GL[:, 0:5], T[lm][:, 0::2], float(TOP), op.min, lm, "GL")
-        tt(T.EX[:, :], T.LF[:, 0:5].indirect(T.LT[:, 0:5]), T.MI[:, 0:80], op.mult, "LF LT MI", "EX")
-        mm(T.b2[0:80, 0:8], T.EX[:, :], T.GSH[:, :], True, True, "EX GSH", "b2")
-        cp(T.GCP[0:80, 0::5], T.b2[0:80, 0:8], "b2", "GCP")
+        sc(T.GT[:, :], T.PT[:, :].indirect(T.JL[:, 0:5]), "PT0 PT1 PT2 PT3 JL", "GT")
+        cp(T.GL[:, 0:5], T[lm][:, 0::2], lm, "GL")
         for i in range(S):
-            mine = step("G", i == S - 1)
-            for pieces in MIX[i]:
+            mine = step("G", i)
+            for pieces in MIX[min(k, 1)][i]:
                 next(mine, None)
                 for _ in range(pieces):
                     next(own, None)
-        ts(T["RT%d" % k][:, 0:5], T.b2[:, 0:5], -rel, op.add, "b2", "RT%d" % k)
+            for _ in mine:
+                pass
+        cp(T["RT%d" % k][:, 0:5], T.b2[:, 0:5], "b2", "RT%d" % k)
         send(lambda q: T["RT%d" % k][:, slot(me, q):slot(me, q) + 1], lambda q: T["RL%d" % k][:, slot(q, me):slot(q, me) + 1], "rt%d" % k, "RT%d" % k)
         event("rt%d" % k, into, "RL%d" % k)
 
     def replies(k):
-        mm(T.b7[:, 128:176], T.ID[:, :], T.CHB[:, :], True, False, "ID CHB", "b7")
+        mm(T.b6[:, 128:176], T.IDS[:, :], T.CHB[:, :], True, False, "IDS CHB", "b6")
         tt(T.RX[:, :], T["RL%d" % k][:, 0:5].indirect(T.LR[:, 0:3]), T.M48[:, :], op.mult, "RL%d LR M48" % k, "RX")
-        mm(T.b7[:, 128:176], T.AT[:, :], T.RX[:, :], False, True, "AT RX", "b7")
-        scan(T.US[:, :], T.R6[:, :], T.b7[:, 128:176], op.mult, op.max, "R6 b7", "US")
+        mm(T.b6[:, 128:176], T.AT[:, :], T.RX[:, :], False, True, "AT RX", "b6")
+        if k < R - 1:
+            scan(T.QI[:, :], T.R6[:, :], T.b6[:, 128:176], op.mult, op.max, "R6 b6", "QI")
+        else:
+            scan(T.US[:, :], T.R6[:, :], T.b6[:, 128:176], op.mult, op.max, "R6 b6", "US")
 
     def to_list():
         tt(T.DX[:, :], T.US[:, :].indirect(T.LA[:, 0:8]), T.MI[:, :], op.mult, "US LA MI", "DX")
-        mm(T.b5[:, 0:8], T.DX[:, :], T.GS[:, :], True, True, "DX GS", "b5")
+        mm(T.b5[:, 0:8], T.DX[:, :], T.GSL[:, :], True, True, "DX GSL", "b5")
 
-    def spread(bank, at, n, src, b):
-        mm(T[bank][:, at:at + n], T.SEL[32 * b:32 * b + 32, :], T[src][32 * b:32 * b + 32, :], True, True, src + " SEL", bank)
-
-    def guest_points():
-        for b, bank in enumerate(("b0", "b1", "b2", "b6")):
-            spread(bank, 0, 160, "PD", b)
-        for b, bank in enumerate(("b0", "b1", "b2", "b6")):
-            do("s", lambda e: e.activation(T.PT[:, 160 * b:160 * b + 160], T[bank][:, 0:160], act.Identity, bias=T.CX[:, 2:3]), bank + " CX2", "PT%d" % b)
-
-    dispatch(0, lambda: ts(T.IA[:, :], T.ICM[:, :], 256.0, op.add, "ICM", "IA"))
-    iota(T.RKI[:, :], [[4, 8], [-1, 5]], 4, 0, "RKI")
-    iota(T.RNI[:, :], [[16, 8], [-1, 5]], 4, 0, "RNI")
-    iota(T.G48[:, :], [[1, 8], [0, 6]], 0, 0, "G48")
-
-    fill(T.SV[:, 3::4], -1000.0, "SV")
-    ts(T.SEL[:, :], T.SV[:, :], p31, op.is_equal, "SV CF", "SEL")
-    for b in range(4):
-        if b:
-            wait("t", "t", count["t"])
-        spread("b3", 32 * b, 32, "P4H", b)
-    ts(T.CX[:, 2:3], p3, 3.0, op.is_equal, "CF", "CX2")
-    do("s", lambda e: e.activation(T.PTH[:, :], T.b3[:, 0:128], act.Identity, bias=T.CX[:, 2:3]), "b3 CX2", "PTH")
+    tt(T.DX[:, :], T.T0I[:, :].indirect(T.LT[:, 0:8]), T.MI[:, :], op.mult, "T0I LT MI", "DX")
+    mm(T.b7[:, 0:8], T.DX[:, :], T.GS[:, :], True, True, "DX GS", "b7")
+    first = constants()
+    for _ in range(GAP0[0]):
+        next(first)
+    ts(T.QI[:, 5::6], T.b7[:, 0:8], 1.0 / TT, op.mult, "b7", "QI", BASE, op.add)
+    for _ in range(GAP0[1]):
+        next(first)
+    ts(T.US[:, 5::6], T.b7[:, 0:8], 1.0 / TT, op.mult, "b7", "US", BASE, op.add)
+    dispatch(0, first)
+    for _ in first:
+        pass
+    ts(T.RN2[:, :], T.RNI[:, :], T.C5[:, 2:3], op.is_equal, "RNI C5", "RN2")
+    tt(T.RNB[:, :], T.RNA[:, :], T.RN2[:, :], op.add, "RNA RN2", "RNB")
     ts(T.IDH[:, :], T.IC[:, :], p, op.is_equal, "IC CF", "IDH")
-    ts(T.ID[:, :], T.IC[:, :], p, op.is_equal, "IC CF", "ID")
-    fill(T.PW[:, 0:OFF], 0, "PWb")
-    fill(T.PW[:, TOP:W], 0, "PWb")
-    fill(T.ON[:, :], 1.0, "ON")
-    cp(T.GSH[:, :], T.GS[:, :], "GS", "GSH")
-    ts(T.LD[:, :], T.IC[:, 0:8], 5.0, op.mult, "IC", "LD", 4.0, op.add)
-    ts(T.HL[:, :], T.T0I[:, :], rel, op.add, "T0I", "HL", float(TOP), op.min)
     hold()
-    ts(T.HCP[:, 0::5], T.US[:, 5::6], rel, op.add, "US", "HCP")
-    hold_own()
-    ts(T.RK[:, 0::2], T.RKI[:, :], p2, op.is_equal, "RKI CF", "RKa", -KEY, op.mult)
-    ts(T.RK[:, 1::2], T.RKI[:, :], p2, op.is_equal, "RKI CF", "RKb", KEY, op.mult)
-    fill(T.RK[:, 0::10], 0.0, "RKa")
-    fill(T.RK[:, 1::10], 0.0, "RKb")
-    ts(T.RN[:, :], T.RNI[:, :], p, op.is_equal, "RNI CF", "RN")
-    fill(T.RN[:, 0::5], 0.0, "RN")
+    turn()
 
+    own, points = home(0), guest_points()
+    next(points)
     for k in range(R):
-        own = home(k)
         for i in range(PRE[min(k, 1)]):
             next(own, None)
-            if i == 1 and k == 0:
-                guest_points()
+            next(points, None)
         guests(k, own)
         if k == 0:
-            ts(T.M48[:, :], T.G48[:, :], pg, op.is_equal, "G48 CF", "M48")
+            ts(T.M48[:, :], T.G48[:, :], pg, op.is_equal, "G48 CF", "M48", 1.0 / TT, op.mult)
             fill(T.M48[:, me::6], 0.0, "M48")
             ts(T.N6F[:, 0:3], T.N6[:, 0:3], -6.0, op.mult, "N6", "N6F")
             tt(T.NM[:, 0:3], T.NI[:, 0:3], T.N6F[:, 0:3], op.add, "NI N6F", "NM")
             ts(T.NG[:, 0:3], T.NM[:, 0:3], float(me), op.is_gt, "NM", "NG")
             tt(T.NK[:, 0:3], T.NM[:, 0:3], T.NG[:, 0:3], op.subtract, "NM NG", "NK")
             ts(T.LR[:, 0:3], T.NK[:, 0:3], 4.0, op.min, "NK", "LR")
+            ts(T.GSL[:, :], T.GS[:, :], float(TT), op.mult, "GS", "GSL")
         for _ in own:
             pass
         replies(k)
         if k < R - 1:
-            dispatch(k + 1)
+            own = home(k + 1)
+            dispatch(k + 1, own)
 
     to_list()
-    cp(T.YS[:, :], T.b5[:, 0:8], "b5", "YS")
+    ts(T.YS[:, :], T.b5[:, 0:8], -TT * BASE, op.add, "b5", "YS")
     dma("y", "sty", T.y[:, :], T.YS[:, :], "YS")
 
     g.wait_ge(T.sem.sty, 16)

from concourse.bass import DstId, RemoteDMATransfer
from concourse.mybir import AluOpType, ActivationFunctionType

N, TT, P, R, S = 6, 1024, 128, 3, 3
OFF = 64
TOP = TT + OFF
W = TOP + 8
FAR = 2048
KEY = 16384.0
BIG = 2.0 ** 37
HOLD = 32768.0
QB = 129
BASE = QB - 1023.0 / 2048
PRE = (2, 3)
MIX = (((2, 1, 0, 0, 2, 0), (2, 1, 1, 0, 2, 0), (2, 1, 4, 7, 5)), ((0, 0, 1, 1, 1, 0), (2, 0, 0, 0, 2, 0), (2, 0, 1, 0, 1)))
GAP0 = (9, 3)
GAP = ((4, 6, 8, 3), (0, 0, 1, 1))


def _s(n, dtype="float32"):
    return ("sbuf", [128, n], dtype)


SCRATCH = {
    "PW": _s(W, "int32"), "NW": _s(W, "bfloat16"), "T0I": _s(8, "int32"),
    "NT": _s(40, "int32"), "NA": _s(40, "int32"), "NU": _s(40), "NP": _s(80, "int32"), "NS": _s(120, "bfloat16"),
    "ND": ("dram", [16, TT], "bfloat16"),
    "P4": _s(32, "int32"), "P4H": _s(32, "float16"), "PD": _s(160, "float16"), "PT": _s(640), "PTH": _s(128),
    "CI": _s(8, "int32"), "CF": _s(8), "C5": _s(3), "CX": _s(4), "IC": _s(128, "int32"), "ICM": _s(128, "int32"),
    "MI": _s(128), "IA": _s(128), "IDS": _s(128), "IDH": _s(128, "float16"), "UT": _s(128, "bfloat16"),
    "GS": _s(8), "GSL": _s(8), "GSH": _s(8, "float16"), "M48": _s(48), "G48": _s(48), "QC": _s(48), "CV": _s(48), "CJ": _s(48), "CJ0": _s(48),
    "RKI": _s(40), "RNI": _s(40), "RK": _s(80), "RN0": _s(40, "bfloat16"), "RN1": _s(40, "bfloat16"), "RN2": _s(40, "bfloat16"),
    "RNA": _s(40, "bfloat16"), "RNB": _s(40, "bfloat16"),
    "CR": _s(80, "bfloat16"), "ON": _s(128, "bfloat16"), "R5": _s(80), "R6": _s(48),
    "SA": _s(128, "int32"), "SB": _s(128, "int32"), "SV": _s(128), "SEL": _s(128, "float16"),
    "NI": _s(4), "N6": _s(4, "int32"), "N6F": _s(4), "NM": _s(4), "NG": _s(4), "NK": _s(4),
    "L6": _s(4, "uint16"), "LR": _s(4, "uint16"), "LA": _s(8, "uint16"), "LD": _s(8, "uint16"), "LT": _s(8, "uint16"),
    "HL": _s(8, "uint16"), "GL": _s(8, "uint16"), "JL": _s(8, "uint16"),
    "US": _s(48), "QI": _s(48, "bfloat16"), "OH": _s(48, "bfloat16"), "VV": _s(48), "BT": _s(96, "float16"), "SS": _s(48),
    "AA": _s(128, "float16"), "AT": _s(128), "M12": _s(12), "MK": _s(24), "TM": _s(24), "CHB": _s(48), "RX": _s(48), "DX": _s(128), "YS": _s(8),
    "GT": _s(80), "GDF": _s(128),
}
for _t in "HG":
    _n = 128 if _t == "H" else 80
    SCRATCH.update({_t + "P": _s(_n), _t + "N": _s(_n, "bfloat16"), _t + "SC": _s(80), _t + "D0": _s(40), _t + "D1": _s(40),
                    _t + "Z": _s(40), _t + "D": _s(128, "float16"), _t + "V0": _s(40 if _t == "G" else 8), _t + "V1": _s(40 if _t == "G" else 8)})
for _k in range(R):
    SCRATCH["MS%d" % _k] = _s(12, "float16")
    SCRATCH["LM%d" % _k] = _s(10, "float16")
    SCRATCH["RT%d" % _k] = _s(8)
    SCRATCH["RL%d" % _k] = _s(8)
for _k in range(8):
    SCRATCH["b%d" % _k] = ("psum", [128, 512], "float32")

SEMAPHORES = ["v", "t", "s", "c", "ltet", "lpts", "lpl", "lnt", "lnd", "lnb", "sty", "pd", "sent"] + ["rq%d" % k for k in range(R)] + ["rt%d" % k for k in range(R)]
BANKS = ["b%d" % k for k in range(8)]


def slot(owner, other):
    return other - (1 if other > owner else 0)


def engine_split(topo, src, dsts):
    on = [d for d in dsts if topo.chip(d) == topo.chip(src)]
    off = [d for d in dsts if topo.chip(d) != topo.chip(src)]
    eo = topo.engines(src, off[0])
    out = {}
    for ds, es in ((off, eo), (on, [e for e in topo.engines(src, on[0]) if e not in eo])):
        per = 1
        while 2 * per * len(ds) <= len(es):
            per *= 2
        for i, d in enumerate(ds):
            out[d] = es[i * per:(i + 1) * per]
    return out


def rank_program(g, core, T, topo):
    me = T.rank_of(core)
    if me is None:
        return
    cores = list(T.cores)
    others = [q for q in range(N) if q != me]
    op = AluOpType
    act = ActivationFunctionType
    rel = float(OFF - TT * me)

    queues = {"v": g.vector, "t": g.tensor, "s": g.scalar, "c": g, "y": g.sync}
    known = {q: {} for q in queues}
    count = {q: 0 for q in queues}
    clocks, writers, readers = {}, {}, {}

    def wait(q, s, n):
        queues[q].wait_ge(T.sem[s], n)
        for a, b in clocks[(s, n)].items():
            known[q][a] = max(b, known[q].get(a, 0))

    def need(q, r, w):
        ev = []
        for k in r:
            ev += writers.get(k, [])
            if k in BANKS:
                ev += [e for e in readers.get(k, []) if e[0] != q]
        for k in w:
            ev += writers.get(k, [])
            ev += [e for e in readers.get(k, []) if e[0] != q]
        top = {}
        for s, n in ev:
            if not (q == "t" and s == "t"):
                top[s] = max(n, top.get(s, 0))
        for s, n in sorted(top.items(), key=lambda e: e[0]):
            if known[q].get(s, 0) >= n:
                continue
            if any(o != s and known[q].get(o, 0) < m and clocks[(o, m)].get(s, 0) >= n for o, m in top.items()):
                continue
            wait(q, s, n)

    def do(q, fn, r, w):
        r, w = r.split(), w.split()
        need(q, r, w)
        fn(queues[q]).then_inc(T.sem[q], 1)
        count[q] += 1
        ev = (q, count[q])
        clocks[ev] = dict(known[q])
        clocks[ev][q] = count[q]
        for k in r:
            readers.setdefault(k, []).append(ev)
        for k in w:
            writers[k] = [ev]
            readers[k] = []

    def event(sem, total, w):
        clocks[(sem, total)] = {sem: total}
        for k in w.split():
            writers[k] = [(sem, total)]
            readers[k] = []

    def dma(q, sem, out, in_, r="", w=""):
        need(q, r.split(), w.split())
        queues[q].dma_start(out, in_).then_inc(T.sem[sem], 16)

    def tt(out, a, b, o, r, w):
        do("v", lambda e: e.tensor_tensor(out=out, in0=a, in1=b, op=o), r, w)

    def ts(out, a, s1, o0, r, w, s2=None, o1=None):
        if o1 is None:
            do("v", lambda e: e.tensor_scalar(out, a, s1, None, op0=o0), r, w)
        else:
            do("v", lambda e: e.tensor_scalar(out, a, s1, s2, op0=o0, op1=o1), r, w)

    def cp(out, a, r, w):
        do("v", lambda e: e.tensor_copy(out, a), r, w)

    def fill(ap, x, w):
        do("v", lambda e: e.memset(ap, x), "", w)

    def sc(out, a, r, w, bias=0.0, scale=1.0, f=act.Copy):
        do("s", lambda e: e.activation(out, a, f, bias=bias, scale=scale), r, w)

    def sfill(ap, n, x, w):
        sc(ap, T.R6[:, 0:n], "R6", w, bias=x, scale=0.0)

    def scan(out, d0, d1, o0, o1, r, w):
        do("v", lambda e: e.tensor_tensor_scan(out, d0, d1, 0.0, o0, o1), r, w)

    def mm(out, lhsT, rhs, start, stop, r, w):
        do("t", lambda e: e.matmul(out, lhsT, rhs, start, stop), r, w)

    def iota(out, pattern, base, cm, w, small=True):
        if small:
            do("c", lambda e: e.iota(out, pattern, base, cm, allow_small_or_imprecise_dtypes=True), "", w)
        else:
            do("c", lambda e: e.iota(out, pattern, base, cm), "", w)

    split = engine_split(topo, core, [cores[q] for q in others])
    into = sum(len(engine_split(topo, cores[q], [c for c in cores if c != cores[q]])[core]) for q in others)
    sent = [0]

    def send(src, dst, sem, r):
        need("c", r.split(), [])
        tr = []
        for q in others:
            rid, pid = topo.addr(cores[q])[:2]
            tr.append(RemoteDMATransfer(dst_ids=[DstId(rid=rid, pnc=pid)], dma_engine_mask=sum(1 << e for e in split[cores[q]]),
                                        remote_sem=T.sem[sem], src=src(q), dst=dst(q)))
            sent[0] += len(split[cores[q]])
        g.remote_dma_fused(tr, local_sem=T.sem.sent)

    fill(T.P4[:, :], 0, "P4")
    dma("y", "ltet", T.T0I[:, :], T.tet0[:, :])
    dma("s", "lnt", T.NT[:, 0:32], T.nbr[:, :])
    for b in range(4):
        dma("y" if b % 2 else "s", "lpts", T.P4[32 * b:32 * b + 24, :], T.pts[:, 32 * b:32 * b + 32], "", "P4")
    for k in range(8):
        dma("y" if k % 2 else "s", "lpl", T.PW[16 * k:16 * k + 16, OFF:TOP], T.planes[:, :])

    fill(T.R6[:, :], 1.0, "R6")
    fill(T.ON[:, :], 1.0, "ON")
    iota(T.CI[:, 0:1], [[0, 1]], 0, 1, "CI0", small=False)
    iota(T.IC[:, :], [[1, 128]], 0, 0, "IC", small=False)
    iota(T.NT[:, 32:40], [[1, 8]], TT * me, 8, "NT1", small=False)
    iota(T.QC[:, :], [[0, 8], [1, 6]], QB, 0, "QC")
    do("c", lambda e: e.affine_select(T.UT[:, :], T.ON[:, :], [[1, 128]], op.is_gt, 0.0, 0, -1), "ON", "UT")
    do("c", lambda e: e.affine_select(T.UT[:, :], T.UT[:, :], [[1, 128]], op.not_equal, 256.0, 0, -1), "UT", "UT")
    iota(T.RKI[:, :], [[4, 8], [-1, 5]], 4, 0, "RKI")
    event("ltet", 16, "T0I")
    event("lnt", 16, "NT0")
    event("lpts", 64, "P4")
    event("lpl", 128, "PWa")

    fill(T.R6[:, 0::6], 0.0, "R6")
    for ap, n, x, w in ((T.GZ[:, :], 40, 0.0, "GZ"), (T.GV0[:, :], 40, 0.0, "GV0"), (T.GV1[:, :], 40, 0.0, "GV1"), (T.R5[:, 0::2], 40, 2 * BIG, "R5"),
                        (T.R5[:, 1::2], 40, KEY / 2, "R5"), (T.R5[:, 0::10], 8, -BIG, "R5"), (T.R5[:, 1::10], 8, -BIG - KEY, "R5"),
                        (T.CR[:, 0::2], 40, KEY / 2, "CR"), (T.CR[:, 1::2], 40, -KEY / 2, "CR"), (T.CR[:, 0::10], 8, 2 * BIG, "CR"),
                        (T.CR[:, 1::10], 8, BIG, "CR")):
        sfill(ap, n, x, w)
    rs, an = op.arith_shift_right, op.bitwise_and
    ts(T.CI[:, 1:2], T.CI[:, 0:1], 15, an, "CI0", "CI1")
    ts(T.CI[:, 2:3], T.CI[:, 0:1], 4, rs, "CI0", "CI2")
    ts(T.CI[:, 3:4], T.CI[:, 0:1], 2, rs, "CI0", "CI3")
    ts(T.CI[:, 4:5], T.CI[:, 0:1], 4, rs, "CI0", "CI4", 1, an)
    ts(T.CI[:, 5:6], T.CI[:, 0:1], 3, an, "CI0", "CI5")
    ts(T.CI[:, 6:7], T.CI[:, 0:1], 5, rs, "CI0", "CI6")
    ts(T.CI[:, 7:8], T.CI[:, 0:1], 31, an, "CI0", "CI7")
    ts(T.ICM[:, :], T.IC[:, :], 15, an, "IC", "ICM")
    cp(T.CF[:, :], T.CI[:, :], "CI0 CI1 CI2 CI3 CI4 CI5 CI6 CI7", "CF")
    p, p15, pg, p2, podd, p3, p5, p31 = [T.CF[:, k:k + 1] for k in range(8)]
    cp(T.LT[:, :], T.IC[:, 0:8], "IC", "LT")
    ts(T.MI[:, :], T.ICM[:, :], p15, op.is_equal, "ICM CF", "MI")
    ts(T.GS[:, :], T.IC[:, 0:8], pg, op.is_equal, "IC CF", "GS")
    ts(T.NI[:, 0:3], T.IC[:, 0:3], 16.0, op.mult, "IC CF", "NI", p15, op.add)
    ts(T.N6[:, 0:3], T.NI[:, 0:3], 1.0 / 6, op.mult, "NI", "N6", -2.5 / 6, op.add)
    ts(T.L6[:, 0:3], T.N6[:, 0:3], 6.0, op.mult, "N6", "L6", 5.0, op.add)

    cp(T.P4H[:, :], T.P4[:, :], "P4", "P4H")
    send(lambda q: T.P4H[:, :], lambda q: T.PD[:, 32 * slot(q, me):32 * slot(q, me) + 32], "pd", "P4H")
    event("pd", into, "PD")
    iota(T.RNI[:, :], [[16, 8], [-1, 5]], 4, 0, "RNI")
    iota(T.C5[:, :], [[-5, 3]], 0, 1, "C5")
    iota(T.G48[:, :], [[1, 8], [0, 6]], 0, 0, "G48")

    def spread(bank, at, n, src, b):
        mm(T[bank][:, at:at + n], T.SEL[32 * b:32 * b + 32, :], T[src][32 * b:32 * b + 32, :], True, True, src + " SEL", bank)

    def guest_points():
        for b, bank in enumerate(("b0", "b1", "b2", "b6")):
            spread(bank, 0, 160, "PD", b)
        for b, bank in ((0, "b0"), (2, "b2")):
            sc(T.PT[:, 160 * b:160 * b + 160], T[bank][:, 0:160], bank + " CX2", "PT%d" % b, bias=T.CX[:, 2:3], f=act.Identity)
        yield
        for b, bank in ((1, "b1"), (3, "b6")):
            ts(T.PT[:, 160 * b:160 * b + 160], T[bank][:, 0:160], T.CX[:, 2:3], op.add, bank + " CX2", "PT%d" % b)
        yield

    def window():
        for b in (1, 2, 0):
            r = "NS%d" % b
            dma("y", "lnd", T.ND[5 * b:5 * b + 4, :], T.NS[:, 40 * b:40 * b + 32], r)
            dma("s", "lnd", T.ND[5 * b + 4:5 * b + 5, :], T.NS[:, 40 * b + 32:40 * b + 40], r)
        dma("y", "lnd", T.ND[15:16, :], T.NS[:, 112:120], "NS2")
        event("lnd", 7 * 16, "ND")
        for k in range(8):
            dma("y", "lnb", T.NW[16 * k:16 * k + 16, OFF:TOP], T.ND[:, :], "ND")
        event("lnb", 128, "NWa")

    def constants():
        fill(T.US[:, :], 0.0, "US")
        yield
        ts(T.NA[:, :], T.NT[:, :], 10, rs, "NT0 NT1", "NA")
        yield
        fill(T.QI[:, :], 0.0, "QI")
        yield
        ts(T.NP[:, 40:80], T.NT[:, :], 63, an, "NT0 NT1", "NP1")
        yield
        ts(T.NU[:, :], T.NA[:, :], float(me), op.is_equal, "NA", "NU", FAR - rel, op.mult)
        yield
        ts(T.NP[:, 0:40], T.NT[:, :], 8192 - 64, an, "NT0 NT1", "NP0")
        yield
        cp(T.NS[:, 40:80], T.NP[:, 40:80], "NP1", "NS1")
        yield
        ts(T.NS[:, 80:120], T.NU[:, :], float(-FAR), op.add, "NU", "NS2")
        yield
        ts(T.CV[:, :], T.QC[:, :], -1.0, op.mult, "QC", "CV", QB - BASE + OFF / float(TT), op.add)
        yield
        ts(T.CJ0[:, :], T.QC[:, :], float(QB + me), op.is_lt, "QC", "CJ0", -32.0, op.mult)
        yield
        tt(T.NS[:, 0:40], T.NP[:, 0:40], T.NS[:, 80:120], op.subtract, "NP0 NS2", "NS0")
        window()
        yield
        ts(T.CX[:, 0:1], p5, 160.0, op.mult, "CF", "CX0", p31, op.add)
        yield
        ts(T.CJ[:, :], T.CJ0[:, :], T.CX[:, 0:1], op.add, "CJ0 CX0", "CJ", 32.0 * me, op.add)
        yield
        ts(T.LA[:, :], T.IC[:, 0:8], 6.0, op.mult, "IC", "LA", 5.0, op.add)
        yield
        ts(T.IA[:, :], T.ICM[:, :], 256.0, op.add, "ICM", "IA")
        yield
        ts(T.SA[:, :], T.IC[:, :], 4, rs, "IC", "SA")
        yield
        ts(T.SB[:, :], T.IC[:, :], 3, an, "IC", "SB")
        yield
        ts(T.SV[:, :], T.SA[:, :], 3.0, op.mult, "SA", "SV")
        yield
        ts(T.CX[:, 1:2], podd, -1.0, op.mult, "CF", "CX1", 1.0, op.add)
        yield
        tt(T.SV[:, :], T.SV[:, :], T.SB[:, :], op.add, "SV SB", "SV")
        yield
        fill(T.M12[:, 0::2], float(TT), "M12a")
        yield
        fill(T.M12[:, 1::2], 1.0, "M12b")
        yield
        fill(T.SV[:, 3::4], -1000.0, "SV")
        yield
        ts(T.MK[:, 0:12], T.M12[:, :], T.CX[:, 1:2], op.mult, "M12a M12b CX1", "MK0")
        yield
        ts(T.MK[:, 12:24], T.M12[:, :], podd, op.mult, "M12a M12b CF", "MK1")
        yield
        ts(T.SEL[:, :], T.SV[:, :], p31, op.is_equal, "SV CF", "SEL")
        yield
        ts(T.CX[:, 2:3], p3, 3.0, op.is_equal, "CF", "CX2")
        for b in range(4):
            if b:
                wait("t", "t", count["t"])
            spread("b3", 32 * b, 32, "P4H", b)
        sc(T.PTH[:, :], T.b3[:, 0:128], "b3 CX2", "PTH", bias=T.CX[:, 2:3], f=act.Identity)
        yield
        ts(T.RK[:, 0::2], T.RKI[:, :], p2, op.is_equal, "RKI CF", "RKa", -KEY, op.mult)
        yield
        ts(T.RK[:, 1::2], T.RKI[:, :], p2, op.is_equal, "RKI CF", "RKb", KEY, op.mult)
        yield
        fill(T.RK[:, 0::10], 0.0, "RKa")
        yield
        fill(T.RK[:, 1::10], 0.0, "RKb")
        yield
        ts(T.HL[:, :], T.T0I[:, :], rel, op.add, "T0I", "HL", float(TOP), op.min)
        yield
        fill(T.PW[:, 0:OFF], 0, "PWb0")
        yield
        fill(T.PW[:, TOP:W], 0, "PWb1")
        yield
        fill(T.NW[:, 0:OFF], 0.0, "NWp0")
        yield
        fill(T.NW[:, TOP:W], 0.0, "NWp1")
        yield
        ts(T.IDS[:, :], T.IC[:, :], p, op.is_equal, "IC CF", "IDS", 1.0 / TT, op.mult)
        yield
        ts(T.RN0[:, :], T.RNI[:, :], T.C5[:, 0:1], op.is_equal, "RNI C5", "RN0")
        yield
        ts(T.RN1[:, :], T.RNI[:, :], T.C5[:, 1:2], op.is_equal, "RNI C5", "RN1")
        yield
        tt(T.RNA[:, :], T.RN0[:, :], T.RN1[:, :], op.add, "RN0 RN1", "RNA")
        yield
        ts(T.GSH[:, :], T.IC[:, 0:8], pg, op.is_equal, "IC CF", "GSH")
        yield
        ts(T.LD[:, :], T.IC[:, 0:8], 5.0, op.mult, "IC", "LD", 4.0, op.add)
        yield

    def dispatch(k, more):
        ms = "MS%d" % k

        def gap(i):
            for _ in range(GAP[min(k, 1)][i]):
                next(more, None)

        tt(T.OH[:, :], T.QI[:, :].indirect(T.L6[:, 0:3]), T.QC[:, :], op.is_equal, "QI L6 QC", "OH")
        mm(T.b7[:, 0:48], T.UT[:, :], T.OH[:, :], True, True, "UT OH", "b7")
        if k:
            scan(T.US[:, :], T.R6[:, :], T.b6[:, 128:176], op.mult, op.max, "R6 b6", "US")
        gap(0)
        tt(T.BT[:, 1::2], T.CJ[:, :], T.OH[:, :], op.mult, "CJ OH", "BTj")
        tt(T.VV[:, :], T.US[:, :].indirect(T.L6[:, 0:3]), T.CV[:, :], op.add, "US L6 CV", "VV")
        scan(T.SS[:, :], T.R6[:, :], T.b7[:, 0:48], op.mult, op.max, "R6 b7", "SS")
        gap(1)
        tt(T.BT[:, 0::2], T.VV[:, :], T.OH[:, :], op.mult, "VV OH", "BTt")
        tt(T.AA[:, :], T.SS[:, :].indirect(T.LA[:, 0:8]), T.IA[:, :], op.is_equal, "SS LA IA", "AA")
        for a in range(4):
            mm(T.b7[32 * a:32 * a + 32, 64:88], T.AA[:, 32 * a:32 * a + 32], T.BT[:, 24 * a:24 * a + 24], True, True, "AA BTj BTt", "b7")
        gap(2)
        tt(T.TM[:, :], T.b7[:, 64:88], T.MK[:, :], op.mult, "b7 MK0 MK1", "TM")
        gap(3)
        tt(T[ms][:, :], T.TM[:, 0:12], T.TM[:, 12:24], op.add, "TM", ms)
        send(lambda q: T[ms][:, 2 * q:2 * q + 2], lambda q: T["LM%d" % k][:, 2 * slot(q, me):2 * slot(q, me) + 2], "rq%d" % k, ms)
        event("rq%d" % k, into, "LM%d" % k)

    def hold():
        ts(T.CHB[:, :], T.OH[:, :], HOLD, op.mult, "OH", "CHB", TT * BASE - HOLD, op.add)

    def turn():
        mm(T.b6[:, 0:128], T.AA[:, :], T.IDH[:, :], True, True, "AA IDH", "b6")
        sc(T.AT[:, :], T.b6[:, 0:128], "b6", "AT")

    def step(h, i):
        last = i == S - 1
        n, lst, pt, bk, bn, bc = (128, T.HL[:, 0:8], "PTH", "b3", "b4", "b5") if h == "H" else (80, T.GL[:, 0:5], "GT", "b0", "b1", "b2")
        ln, m = h + "L", n // 16
        X = lambda a: T[h + a]
        ones = lambda: mm(T[bk][0:n, 0:80], T.ON[0:1, 0:n], T.CR[0:1, :], True, False, "ON CR", bk)
        left = lambda j: mm(T[bn][0:n, 0:40], T.IDS[0:n, 0:n], X("V%d" % j)[0:n, :], not j, False, "IDS " + h + "V%d" % j, bn)
        if not i:
            ones()
        sc(X("N")[:, :], T.NW[:, :].indirect(lst), "NWp0 NWp1 NWa " + ln, h + "N")
        tt(X("P")[:, :], T.PW[:, :].indirect(lst), T[pt][:, 0:n], op.mult, "PWa PWb0 PWb1 " + ln + " " + pt, h + "P")
        mm(T[bk][0:n, 0:80], X("P")[:, :], T.RK[:, :], False, True, h + "P RKa RKb", bk)
        if last:
            mm(T[bn][0:n, 0:40], X("N")[:, :], T.RNB[:, :], h == "H", True, h + "N RNB", bn)
        else:
            mm(T[bn][0:n, 0:40], X("N")[:, :], T.RNA[:, :], True, True, h + "N RNA", bn)
        yield
        scan(X("SC")[0:n, :], T.R5[0:n, :], T[bk][0:n, 0:80], op.min, op.add, "R5 " + bk, h + "SC")
        if h == "G":
            sc(X("D0")[0:n, :], X("SC")[0:n, 0::2], h + "SC", h + "D0", scale=-1.0)
        if not last:
            ones()
        yield
        tt(X("D1")[0:n, :], X("SC")[0:n, 0::2], T[bn][0:n, 0:40], op.min, h + "SC " + bn, h + "D1")
        if h == "H":
            ts(X("D0")[0:n, :], X("SC")[0:n, 0::2], -1.0, op.mult, h + "SC", h + "D0")
        if h == "G" and i == S - 2:
            left(0)
        yield
        if h == "H" and i:
            tt(T.CHB[:, me::6], T.CHB[:, me::6], T["HV%d" % (i - 1)][:, :], op.add, "CHB HV%d" % (i - 1), "CHB")
        scan(X("Z")[0:n, :], X("D0")[0:n, :], X("D1")[0:n, :], op.min, op.max, h + "D0 " + h + "D1", h + "Z")
        yield
        if not last:
            v, c = (T["HV%d" % i][:, :], 1) if h == "H" else (T["GV%d" % i][0:n, 0::5], TT)
            sc(v, X("Z")[0:n, 4::5], h + "Z", h + "V%d" % i, bias=float(-FAR * c), scale=float(c), f=act.Relu)
            tt(X("D")[:, :], X("Z")[:, :].indirect(T.LD[:, 0:8]), T.MI[:, :], op.mult, h + "Z LD MI", h + "D")
            mm(T[bc][:, 0:m], X("D")[0:n, :], T.GSH[0:n, 0:m], True, True, h + "D GSH", bc)
            if h == "G" and i == S - 2:
                left(1)
            yield
            ts(lst, T[bc][:, 0:m], float(TOP), op.min, bc, ln)
            yield
        elif h == "H":
            tt(T.CHB[:, me::6], T.CHB[:, me::6], T.HZ[:, 4::5], op.add, "CHB HZ", "CHB")
            yield
        else:
            tt(T.GDF[:, :], T.GZ[:, :].indirect(T.LD[:, 0:8]), T.MI[:, :], op.mult, "GZ LD MI", "GDF")
            mm(T[bc][:, 0:m], T.GDF[0:n, :], T.GS[0:n, 0:m], True, True, "GDF GS", bc)
            yield

    def home(k):
        if k:
            to_list()
            yield
            hold()
            turn()
            yield
            ts(T.HL[:, :], T.b5[:, 0:8], rel - TT * BASE, op.add, "b5", "HL", float(TOP), op.min)
            yield
        for i in range(S):
            for _ in step("H", i):
                yield

    def guests(k, own):
        lm = "LM%d" % k
        cp(T.JL[:, 0:5], T[lm][:, 1::2], lm, "JL")
        sc(T.GT[:, :], T.PT[:, :].indirect(T.JL[:, 0:5]), "PT0 PT1 PT2 PT3 JL", "GT")
        cp(T.GL[:, 0:5], T[lm][:, 0::2], lm, "GL")
        for i in range(S):
            mine = step("G", i)
            for pieces in MIX[min(k, 1)][i]:
                next(mine, None)
                for _ in range(pieces):
                    next(own, None)
            for _ in mine:
                pass
        cp(T["RT%d" % k][:, 0:5], T.b2[:, 0:5], "b2", "RT%d" % k)
        send(lambda q: T["RT%d" % k][:, slot(me, q):slot(me, q) + 1], lambda q: T["RL%d" % k][:, slot(q, me):slot(q, me) + 1], "rt%d" % k, "RT%d" % k)
        event("rt%d" % k, into, "RL%d" % k)

    def replies(k):
        mm(T.b6[:, 128:176], T.IDS[:, :], T.CHB[:, :], True, False, "IDS CHB", "b6")
        tt(T.RX[:, :], T["RL%d" % k][:, 0:5].indirect(T.LR[:, 0:3]), T.M48[:, :], op.mult, "RL%d LR M48" % k, "RX")
        mm(T.b6[:, 128:176], T.AT[:, :], T.RX[:, :], False, True, "AT RX", "b6")
        if k < R - 1:
            scan(T.QI[:, :], T.R6[:, :], T.b6[:, 128:176], op.mult, op.max, "R6 b6", "QI")
        else:
            scan(T.US[:, :], T.R6[:, :], T.b6[:, 128:176], op.mult, op.max, "R6 b6", "US")

    def to_list():
        tt(T.DX[:, :], T.US[:, :].indirect(T.LA[:, 0:8]), T.MI[:, :], op.mult, "US LA MI", "DX")
        mm(T.b5[:, 0:8], T.DX[:, :], T.GSL[:, :], True, True, "DX GSL", "b5")

    tt(T.DX[:, :], T.T0I[:, :].indirect(T.LT[:, 0:8]), T.MI[:, :], op.mult, "T0I LT MI", "DX")
    mm(T.b7[:, 0:8], T.DX[:, :], T.GS[:, :], True, True, "DX GS", "b7")
    first = constants()
    for _ in range(GAP0[0]):
        next(first)
    ts(T.QI[:, 5::6], T.b7[:, 0:8], 1.0 / TT, op.mult, "b7", "QI", BASE, op.add)
    for _ in range(GAP0[1]):
        next(first)
    ts(T.US[:, 5::6], T.b7[:, 0:8], 1.0 / TT, op.mult, "b7", "US", BASE, op.add)
    dispatch(0, first)
    for _ in first:
        pass
    ts(T.RN2[:, :], T.RNI[:, :], T.C5[:, 2:3], op.is_equal, "RNI C5", "RN2")
    tt(T.RNB[:, :], T.RNA[:, :], T.RN2[:, :], op.add, "RNA RN2", "RNB")
    ts(T.IDH[:, :], T.IC[:, :], p, op.is_equal, "IC CF", "IDH")
    hold()
    turn()

    own, points = home(0), guest_points()
    next(points)
    for k in range(R):
        for i in range(PRE[min(k, 1)]):
            next(own, None)
            next(points, None)
        guests(k, own)
        if k == 0:
            ts(T.M48[:, :], T.G48[:, :], pg, op.is_equal, "G48 CF", "M48", 1.0 / TT, op.mult)
            fill(T.M48[:, me::6], 0.0, "M48")
            ts(T.N6F[:, 0:3], T.N6[:, 0:3], -6.0, op.mult, "N6", "N6F")
            tt(T.NM[:, 0:3], T.NI[:, 0:3], T.N6F[:, 0:3], op.add, "NI N6F", "NM")
            ts(T.NG[:, 0:3], T.NM[:, 0:3], float(me), op.is_gt, "NM", "NG")
            tt(T.NK[:, 0:3], T.NM[:, 0:3], T.NG[:, 0:3], op.subtract, "NM NG", "NK")
            ts(T.LR[:, 0:3], T.NK[:, 0:3], 4.0, op.min, "NK", "LR")
            ts(T.GSL[:, :], T.GS[:, :], float(TT), op.mult, "GS", "GSL")
        for _ in own:
            pass
        replies(k)
        if k < R - 1:
            own = home(k + 1)
            dispatch(k + 1, own)

    to_list()
    ts(T.YS[:, :], T.b5[:, 0:8], -TT * BASE, op.add, "b5", "YS")
    dma("y", "sty", T.y[:, :], T.YS[:, :], "YS")

    g.wait_ge(T.sem.sty, 16)
    g.wait_ge(T.sem.sent, sent[0])
    for q in "vtsc":
        if known["c"].get(q, 0) < count[q]:
            g.wait_ge(T.sem[q], count[q])
